import numpy as np
import ml_dtypes


def mxq(x, axis, fmt="e4m3"):
    dtype, down = {"e4m3": (ml_dtypes.float8_e4m3fn, 7), "e5m2": (ml_dtypes.float8_e5m2, 14)}[fmt]
    v = np.moveaxis(np.asarray(x, np.float32).astype(ml_dtypes.bfloat16).astype(np.float64), axis, -1)
    blocks = v.reshape(v.shape[:-1] + (-1, 32))
    amax = np.abs(blocks).max(-1, keepdims=True)
    byte = np.maximum(np.where(amax > 0, np.frexp(amax)[1] - 1 + 127, 0) - down, 1)
    scale = np.exp2(byte - 127.0)
    codes = (blocks / scale).astype(np.float32).astype(dtype).astype(np.float64)
    return np.moveaxis((codes * scale).reshape(v.shape), -1, axis)


WIDE = False


def mx_kscale(k):
    if not WIDE:
        return np.ones(k)
    levels = np.array([10, -10, 5, -5, 0])
    if k % 512:
        return np.exp2(np.random.permutation(np.resize(levels, k // 32))).repeat(32)
    a = np.empty((k // 512, 16))
    for p in range(k // 512):
        a[p, :8] = np.random.permutation(np.resize(levels, 8))
        for g in range(8):
            far = levels[np.abs(levels - a[p, g]) >= 10]
            a[p, g + 8] = far[np.random.randint(len(far))]
    return np.exp2(a.ravel()).repeat(32)


def f64(x):
    return np.asarray(x).astype(np.float64)


def striped(idx):
    return np.tile(idx.reshape(-1, 16).T, (8, 1)).astype(np.uint16)


def unstriped(offs):
    return offs[:16].T.reshape(-1).astype(np.int64)


def striped8(idx):
    return np.concatenate([x.reshape(-1, 16).T for x in idx]).astype(np.uint16)


def runs(offs, k):
    lists = np.stack([offs[16 * r : 16 * r + 16].T.reshape(-1) for r in range(8)]).astype(np.int64)
    return lists[np.arange(k) % 512 // 64]


def pack_weight(w):
    k, n = w.shape
    w = f64(np.asarray(w, np.float32).astype(ml_dtypes.bfloat16)).reshape(k // 32, 32, n)
    amax = np.abs(w).max(1)
    byte = np.clip(np.where(amax > 0, np.frexp(amax)[1] - 1 + 127 - 7, 1), 1, 254)
    scaled = (w * np.exp2(127.0 - byte)[:, None, :]).reshape(k, n).astype(np.float32)
    words = np.ascontiguousarray(scaled.reshape(k // 512, 128, 4, n).transpose(0, 1, 3, 2)).astype(ml_dtypes.float8_e4m3fn).view(np.uint8)
    return words, np.ascontiguousarray(byte.astype(np.uint8).reshape(k // 512, 16, n))


def unpack_weight(words, scales):
    g, p, n, _ = words.shape
    vals = np.ascontiguousarray(words).view(ml_dtypes.float8_e4m3fn).astype(np.float64) * np.repeat(np.exp2(scales.astype(np.float64) - 127.0), 8, axis=1)[..., None]
    return vals.transpose(0, 1, 3, 2).reshape(g * 512, n)


def gelu(v):
    return 0.5 * v * (1.0 + np.tanh(np.sqrt(2.0 / np.pi) * (v + 0.044715 * v**3)))

def planes(y):
    n, m = y.shape
    v = y.astype(np.float32).astype(ml_dtypes.bfloat16).astype(np.float64).reshape(n // 32, 32, m)
    top = np.abs(v).max(1)
    byte = np.clip(np.where(top > 0, np.frexp(top)[1] - 1 + 127 - 7, 1), 1, 254)
    codes = (v * np.exp2(127.0 - byte)[:, None, :]).reshape(n, m).astype(np.float32).astype(ml_dtypes.float8_e4m3fn).view(np.uint8)
    words = codes.reshape(n // 512, 128, 4, m).transpose(0, 1, 3, 2)
    return np.ascontiguousarray(words), np.ascontiguousarray(byte.astype(np.uint8).reshape(n // 512, 16, m))


K, T, S, V, N, H = 512, 2048, 512, 256, 512, 512


def setup_inputs():
    n = np.random.standard_normal
    s = mx_kscale(K)[:, None]
    u = mx_kscale(H)
    packed_xT = pack_weight(n((K, T)) * s)
    packed_w2 = pack_weight(n((H, N)) / np.sqrt(H) / u[:, None])
    return {
        "x_words": packed_xT[0],
        "x_scales": packed_xT[1],
        "w1": (n((K, H)) / np.sqrt(K) / s * u).astype(np.float32),
        "w2_words": packed_w2[0],
        "w2_scales": packed_w2[1],
        "offs": striped(np.random.permutation(T)[:S]),
        "src": striped8(np.stack([np.random.permutation(S)[:V] for _ in range(8)])),
        "dst": striped8(np.stack([np.random.permutation(S)[:V] for _ in range(8)])),
    }


def reference(x_words, x_scales, w1, w2_words, w2_scales, offs, src, dst):
    xq = unpack_weight(x_words, x_scales)[:, unstriped(offs)]
    y = mxq(f64(w1), 0, "e4m3").T @ xq
    m1 = gelu(y[np.arange(H)[:, None], runs(src, H)])
    z = y.copy()
    z[np.arange(H)[:, None], runs(dst, H)] = m1
    out_0 = unpack_weight(w2_words, w2_scales).T @ mxq(z, 0, "e4m3")
    return (out_0,) + planes(out_0)

@@ -1,0 +1,184 @@
+from contextlib import ExitStack
+
+import concourse.mybir as mybir
+
+K, T, S, V, N, H = 512, 2048, 512, 256, 512, 512
+FLOPS = 2 * K * H * S + 2 * H * N * S
+
+F32 = mybir.dt.float32
+BF16 = mybir.dt.bfloat16
+I32 = mybir.dt.int32
+U32 = mybir.dt.uint32
+U16 = mybir.dt.uint16
+U8 = mybir.dt.uint8
+FP8X4 = mybir.dt.float8_e4m3fn_x4
+GELU = mybir.ActivationFunctionType.Gelu_apprx_tanh
+
+P = 128
+PACK = 4
+HALF = S // 2
+CHUNK = 128
+CHUNKS = S // CHUNK
+
+
+def as_words(packed):
+    return packed[0].rearrange("p n t -> p (n t)").bitcast(I32)
+
+
+def load_scale_rows(queue, plane, scales):
+    for q in range(4):
+        queue.dma_start(out=plane[32 * q : 32 * q + 4, :].bitcast(I32), in_=scales[0, 4 * q : 4 * q + 4, :].bitcast(I32))
+
+
+def tile_picked_deliver_gelu_po_kernel(
+    tc, x_words, x_scales, w1, w2_words, w2_scales, offs, src, dst, out_0, out_1, out_2
+):
+    nc = tc.nc
+    with ExitStack() as ctx:
+        sb = ctx.enter_context(tc.tile_pool(name="sb", bufs=1))
+        psum = ctx.enter_context(tc.psum_pool(name="psum", bufs=1))
+
+        offs_sb = sb.tile([P, S // 16], U16, name="offs_sb")
+        src_sb = sb.tile([P, V // 16], U16, name="src_sb")
+        dst_sb = sb.tile([P, V // 16], U16, name="dst_sb")
+        x_table = sb.tile([P, T], I32, name="x_table", align_bytes=64)
+        x_table_scales = sb.tile([P, T], U8, name="x_table_scales", align_bytes=64)
+        w2_raw = sb.tile([P, N], I32, name="w2_raw", align_bytes=64)
+        w2_raw_scales = sb.tile([P, N], U8, name="w2_raw_scales", align_bytes=64)
+        w1_raw = [sb.tile([P, PACK, H // 2], F32, name=f"w1_raw{u}", align_bytes=64) for u in range(2)]
+        warm = sb.tile([P, 8], F32, name="warm")
+        warm_out = sb.tile([P, 8], F32, name="warm_out")
+
+        nc.vector.memset(x_table_scales[:].bitcast(I32), 0)
+        nc.vector.memset(warm[:], 0.0)
+        nc.vector.memset(w2_raw_scales[:].bitcast(I32), 0)
+
+        w1_rows = w1.rearrange("(p j) c -> p j c", j=PACK)
+        nc.sync.dma_start(offs_sb[:], offs)
+        nc.scalar.activation(warm_out[:], warm[:], GELU)
+        nc.sync.dma_start(out=w1_raw[0][:], in_=w1_rows[:, :, 0 : H // 2])
+        load_scale_rows(nc.sync, x_table_scales, x_scales)
+        nc.sync.dma_start(out=w1_raw[1][:], in_=w1_rows[:, :, H // 2 : H])
+        nc.sync.dma_start(out=x_table[:], in_=as_words(x_words))
+        nc.sync.dma_start(out=w2_raw[:], in_=as_words(w2_words))
+        nc.sync.dma_start(src_sb[:], src)
+        nc.sync.dma_start(dst_sb[:], dst)
+        load_scale_rows(nc.sync, w2_raw_scales, w2_scales)
+
+        w1_bf = sb.tile([P, PACK, P, PACK], BF16, name="w1_bf", align_bytes=64)
+        for u in range(2):
+            nc.scalar.copy(
+                out=w1_bf[:, :, u * 64 : (u + 1) * 64, :].rearrange("p t m j -> p m t j"),
+                in_=w1_raw[u][:].rearrange("p j (m t) -> p m t j", t=PACK),
+            )
+        x_scale = sb.tile([P, S], U8, name="x_scale", align_bytes=64)
+        nc.vector.tensor_copy(x_scale[:], x_table_scales[:].indirect(offs_sb[:]))
+        w1_codes = sb.tile([P, H], U32, name="w1_codes", align_bytes=64)
+        w1_scale = sb.tile([P, H], U8, name="w1_scale", align_bytes=64)
+        nc.vector.quantize_mx(out=w1_codes[:].bitcast(FP8X4), scales=w1_scale[:], in_=w1_bf[:].rearrange("p t m j -> p (t m j)"))
+
+        x_codes = [sb.tile([P, HALF], U32, name=f"x_codes{h}", align_bytes=64) for h in range(2)]
+        for h in range(2):
+            nc.vector.tensor_copy(x_codes[h][:], x_table[:].bitcast(U32).indirect(offs_sb[:, h * 16 : (h + 1) * 16]))
+
+        order = [2, 0, 1, 3]
+        z = [sb.tile([P, S], F32, name=f"z{t}", tag=f"z{t}", align_bytes=64) for t in range(PACK)]
+
+        def first_product(acc, t, h):
+            nc.tensor.matmul_mx(
+                out=acc,
+                lhsT=w1_codes[:, t * P : (t + 1) * P].bitcast(FP8X4),
+                lhsT_scale=w1_scale[:, t * P : (t + 1) * P],
+                rhs=x_codes[h][:].bitcast(FP8X4),
+                rhs_scale=x_scale[:, h * HALF : (h + 1) * HALF],
+                start=True,
+                stop=True,
+            )
+
+        lead = [psum.tile([P, HALF], F32, name=f"lead{h}", tag=f"bank{h}") for h in range(2)]
+        rest = [psum.tile([P, S], F32, name=f"rest{i}", tag=f"bank{2 + i}") for i in range(3)]
+        first_product(lead[0][:], order[0], 0)
+        first_product(rest[0][:, 0:HALF], order[1], 0)
+        first_product(lead[1][:], order[0], 1)
+        first_product(rest[0][:, HALF:S], order[1], 1)
+        for i in (1, 2):
+            for h in range(2):
+                first_product(rest[i][:, h * HALF : (h + 1) * HALF], order[i + 1], h)
+        for h in range(2):
+            nc.scalar.copy(out=z[order[0]][:, h * HALF : (h + 1) * HALF], in_=lead[h][:])
+        for i in range(3):
+            nc.scalar.copy(out=z[order[i + 1]][:], in_=rest[i][:])
+
+        w2_codes = sb.tile([P, N], I32, name="w2_codes", align_bytes=64)
+        w2_scale = sb.tile([P, N], U8, name="w2_scale", align_bytes=64)
+        nc.vector.tensor_copy(
+            out=w2_codes[:].rearrange("p (t m) -> p t m", t=PACK), in_=w2_raw[:].rearrange("p (m t) -> p t m", t=PACK)
+        )
+        nc.vector.tensor_copy(
+            out=w2_scale[:].rearrange("p (t m) -> p t m", t=PACK), in_=w2_raw_scales[:].rearrange("p (m t) -> p t m", t=PACK)
+        )
+
+        fetched = [sb.tile([P, V], F32, name=f"fetched{t}", align_bytes=64) for t in range(PACK)]
+        last = order[3]
+        for t in order:
+            nc.vector.tensor_copy(fetched[t][:], z[t][:].indirect(src_sb[:]))
+        message = {t: sb.tile([P, V], F32, name=f"message{t}", align_bytes=64) for t in order[:3]}
+        for t in order[:3]:
+            nc.scalar.activation(message[t][:], fetched[t][:], GELU)
+        z_bf = sb.tile([P, S, PACK], BF16, name="z_bf", align_bytes=64)
+        for t in order[:3]:
+            nc.vector.tensor_copy(z[t][:].indirect(dst_sb[:]), message[t][:])
+        nc.scalar.copy(out=z_bf[:, :, order[0]], in_=z[order[0]][:])
+        last_message = sb.tile([P, V], F32, name="last_message", tag=f"z{order[0]}", align_bytes=64)
+        nc.scalar.activation(last_message[:], fetched[last][:], GELU)
+        nc.vector.tensor_copy(z[last][:].indirect(dst_sb[:]), last_message[:])
+        for t in order[1:3]:
+            nc.scalar.copy(out=z_bf[:, :, t], in_=z[t][:])
+        for c in range(CHUNKS):
+            cols = slice(c * CHUNK, (c + 1) * CHUNK)
+            if c < 2:
+                nc.vector.tensor_copy(out=z_bf[:, cols, last], in_=z[last][:, cols])
+            else:
+                nc.scalar.copy(out=z_bf[:, cols, last], in_=z[last][:, cols])
+
+        z_codes = sb.tile([P, S], U32, name="z_codes", align_bytes=64)
+        z_scale = sb.tile([P, S], U8, name="z_scale", align_bytes=64)
+        for c in range(CHUNKS):
+            cols = slice(c * CHUNK, (c + 1) * CHUNK)
+            nc.vector.quantize_mx(
+                out=z_codes[:, cols].bitcast(FP8X4), scales=z_scale[:, cols], in_=z_bf[:, cols, :].rearrange("p n t -> p (n t)")
+            )
+
+        out_rows = out_0.rearrange("(p t) n -> p t n", t=PACK)
+        out_words = as_words(out_1)
+        out_codes = sb.tile([P, S], I32, name="out_codes", align_bytes=64)
+        out_scale = sb.tile([P, S], U8, name="out_scale", align_bytes=64)
+        for c in range(CHUNKS):
+            cols = slice(c * CHUNK, (c + 1) * CHUNK)
+            acc = psum.tile([P, PACK, CHUNK], F32, name=f"acc{c}", tag=f"bank{(5 + c) % 8}")
+            for t in range(PACK):
+                nc.tensor.matmul_mx(
+                    out=acc[:, t, :],
+                    lhsT=w2_codes[:, t * P : (t + 1) * P].bitcast(FP8X4),
+                    lhsT_scale=w2_scale[:, t * P : (t + 1) * P],
+                    rhs=z_codes[:, cols].bitcast(FP8X4),
+                    rhs_scale=z_scale[:, cols],
+                    start=True,
+                    stop=True,
+                )
+            result = sb.tile([P, PACK, CHUNK], F32, name=f"result{c}", align_bytes=64)
+            nc.scalar.copy(out=result[:], in_=acc[:])
+            nc.sync.dma_start(out=out_rows[:, :, cols], in_=result[:])
+            result_bf = sb.tile([P, CHUNK, PACK], BF16, name=f"result_bf{c}", align_bytes=64)
+            nc.vector.tensor_copy(
+                out=result_bf[:].rearrange("p (a i) t -> p a t i", i=4), in_=result[:].rearrange("p t (a i) -> p a t i", i=4)
+            )
+            nc.vector.quantize_mx(
+                out=out_codes[:, cols].bitcast(FP8X4), scales=out_scale[:, cols], in_=result_bf[:].rearrange("p n t -> p (n t)")
+            )
+            if c % 2 == 1:
+                pair = slice((c - 1) * CHUNK, (c + 1) * CHUNK)
+                nc.sync.dma_start(out=out_words[:, pair], in_=out_codes[:, pair])
+        for q in range(4):
+            queue = nc.scalar if q % 2 else nc.sync
+            queue.dma_start(out=out_2[0, 4 * q : 4 * q + 4, :].bitcast(I32), in_=out_scale[32 * q : 32 * q + 4, :].bitcast(I32))

@@ -43,36 +43,37 @@ def tile_picked_deliver_gelu_po_kernel(
         dst_sb = sb.tile([P, V // 16], U16, name="dst_sb")
         x_table = sb.tile([P, T], I32, name="x_table", align_bytes=64)
         x_table_scales = sb.tile([P, T], U8, name="x_table_scales", align_bytes=64)
-        w2_raw = sb.tile([P, N], I32, name="w2_raw", align_bytes=64)
-        w2_raw_scales = sb.tile([P, N], U8, name="w2_raw_scales", align_bytes=64)
+        w2_raw = sb.tile([P, N], I32, name="w2_raw", tag="w2_raw", align_bytes=64)
+        w2_raw_scales = sb.tile([P, N], U8, name="w2_raw_scales", tag="w2_raw_scales", align_bytes=64)
         w1_raw = [sb.tile([P, PACK, H // 2], F32, name=f"w1_raw{u}", align_bytes=64) for u in range(2)]
         warm = sb.tile([P, 8], F32, name="warm")
         warm_out = sb.tile([P, 8], F32, name="warm_out")
 
         nc.vector.memset(x_table_scales[:].bitcast(I32), 0)
         nc.vector.memset(warm[:], 0.0)
-        nc.vector.memset(w2_raw_scales[:].bitcast(I32), 0)
+        nc.gpsimd.memset(w2_raw_scales[:].bitcast(I32), 0)
 
         w1_rows = w1.rearrange("(p j) c -> p j c", j=PACK)
-        nc.sync.dma_start(offs_sb[:], offs)
         nc.scalar.activation(warm_out[:], warm[:], GELU)
         nc.sync.dma_start(out=w1_raw[0][:], in_=w1_rows[:, :, 0 : H // 2])
         load_scale_rows(nc.sync, x_table_scales, x_scales)
+        nc.sync.dma_start(offs_sb[:], offs)
         nc.sync.dma_start(out=w1_raw[1][:], in_=w1_rows[:, :, H // 2 : H])
         nc.sync.dma_start(out=x_table[:], in_=as_words(x_words))
         nc.sync.dma_start(out=w2_raw[:], in_=as_words(w2_words))
+        load_scale_rows(nc.sync, w2_raw_scales, w2_scales)
         nc.sync.dma_start(src_sb[:], src)
         nc.sync.dma_start(dst_sb[:], dst)
-        load_scale_rows(nc.sync, w2_raw_scales, w2_scales)
 
         w1_bf = sb.tile([P, PACK, P, PACK], BF16, name="w1_bf", align_bytes=64)
+        x_scale = sb.tile([P, S], U8, name="x_scale", align_bytes=64)
         for u in range(2):
-            nc.scalar.copy(
+            nc.vector.tensor_copy(
                 out=w1_bf[:, :, u * 64 : (u + 1) * 64, :].rearrange("p t m j -> p m t j"),
                 in_=w1_raw[u][:].rearrange("p j (m t) -> p m t j", t=PACK),
             )
-        x_scale = sb.tile([P, S], U8, name="x_scale", align_bytes=64)
-        nc.vector.tensor_copy(x_scale[:], x_table_scales[:].indirect(offs_sb[:]))
+            if u == 0:
+                nc.vector.tensor_copy(x_scale[:], x_table_scales[:].indirect(offs_sb[:]))
         w1_codes = sb.tile([P, H], U32, name="w1_codes", align_bytes=64)
         w1_scale = sb.tile([P, H], U8, name="w1_scale", align_bytes=64)
         nc.vector.quantize_mx(out=w1_codes[:].bitcast(FP8X4), scales=w1_scale[:], in_=w1_bf[:].rearrange("p t m j -> p (t m j)"))
@@ -112,31 +113,33 @@ def tile_picked_deliver_gelu_po_kernel(
         w2_codes = sb.tile([P, N], I32, name="w2_codes", align_bytes=64)
         w2_scale = sb.tile([P, N], U8, name="w2_scale", align_bytes=64)
         nc.vector.tensor_copy(
-            out=w2_codes[:].rearrange("p (t m) -> p t m", t=PACK), in_=w2_raw[:].rearrange("p (m t) -> p t m", t=PACK)
+            out=w2_codes[:].rearrange("p (t m) -> p m t", t=PACK), in_=w2_raw[:].rearrange("p (m t) -> p m t", t=PACK)
         )
         nc.vector.tensor_copy(
-            out=w2_scale[:].rearrange("p (t m) -> p t m", t=PACK), in_=w2_raw_scales[:].rearrange("p (m t) -> p t m", t=PACK)
+            out=w2_scale[:].rearrange("p (t m) -> p m t", t=PACK), in_=w2_raw_scales[:].rearrange("p (m t) -> p m t", t=PACK)
         )
 
-        fetched = [sb.tile([P, V], F32, name=f"fetched{t}", align_bytes=64) for t in range(PACK)]
+        fetched = [
+            sb.tile([P, V], F32, name=f"fetched{t}", tag={order[0]: "w2_raw", order[1]: "w2_raw_scales"}.get(t, f"fetched{t}"), align_bytes=64)
+            for t in range(PACK)
+        ]
         last = order[3]
         for t in order:
             nc.vector.tensor_copy(fetched[t][:], z[t][:].indirect(src_sb[:]))
-        message = {t: sb.tile([P, V], F32, name=f"message{t}", align_bytes=64) for t in order[:3]}
-        for t in order[:3]:
+        message = {t: sb.tile([P, V], F32, name=f"message{t}", align_bytes=64) for t in order}
+        for t in order:
             nc.scalar.activation(message[t][:], fetched[t][:], GELU)
         z_bf = sb.tile([P, S, PACK], BF16, name="z_bf", align_bytes=64)
-        for t in order[:3]:
+        for t in order:
             nc.vector.tensor_copy(z[t][:].indirect(dst_sb[:]), message[t][:])
-        nc.scalar.copy(out=z_bf[:, :, order[0]], in_=z[order[0]][:])
-        last_message = sb.tile([P, V], F32, name="last_message", tag=f"z{order[0]}", align_bytes=64)
-        nc.scalar.activation(last_message[:], fetched[last][:], GELU)
-        nc.vector.tensor_copy(z[last][:].indirect(dst_sb[:]), last_message[:])
-        for t in order[1:3]:
-            nc.scalar.copy(out=z_bf[:, :, t], in_=z[t][:])
+        nc.scalar.copy(out=z_bf[:, 0:CHUNK, 2:4], in_=z[order[0]][:, 0:CHUNK].rearrange("p (n o) -> p n o", o=1).to_broadcast([P, CHUNK, 2]))
+        nc.scalar.copy(out=z_bf[:, CHUNK:S, order[0]], in_=z[order[0]][:, CHUNK:S])
+        nc.scalar.copy(out=z_bf[:, :, order[1]], in_=z[order[1]][:])
+        for h in range(2):
+            nc.scalar.copy(out=z_bf[:, h * HALF : (h + 1) * HALF, order[2]], in_=z[order[2]][:, h * HALF : (h + 1) * HALF])
         for c in range(CHUNKS):
             cols = slice(c * CHUNK, (c + 1) * CHUNK)
-            if c < 2:
+            if c == 0:
                 nc.vector.tensor_copy(out=z_bf[:, cols, last], in_=z[last][:, cols])
             else:
                 nc.scalar.copy(out=z_bf[:, cols, last], in_=z[last][:, cols])
@@ -153,29 +156,39 @@ def tile_picked_deliver_gelu_po_kernel(
         out_words = as_words(out_1)
         out_codes = sb.tile([P, S], I32, name="out_codes", align_bytes=64)
         out_scale = sb.tile([P, S], U8, name="out_scale", align_bytes=64)
+        result_bf = sb.tile([P, S, PACK], BF16, name="result_bf", align_bytes=64)
         for c in range(CHUNKS):
             cols = slice(c * CHUNK, (c + 1) * CHUNK)
-            acc = psum.tile([P, PACK, CHUNK], F32, name=f"acc{c}", tag=f"bank{(5 + c) % 8}")
-            for t in range(PACK):
-                nc.tensor.matmul_mx(
-                    out=acc[:, t, :],
-                    lhsT=w2_codes[:, t * P : (t + 1) * P].bitcast(FP8X4),
-                    lhsT_scale=w2_scale[:, t * P : (t + 1) * P],
-                    rhs=z_codes[:, cols].bitcast(FP8X4),
-                    rhs_scale=z_scale[:, cols],
-                    start=True,
-                    stop=True,
-                )
             result = sb.tile([P, PACK, CHUNK], F32, name=f"result{c}", align_bytes=64)
-            nc.scalar.copy(out=result[:], in_=acc[:])
-            nc.sync.dma_start(out=out_rows[:, :, cols], in_=result[:])
-            result_bf = sb.tile([P, CHUNK, PACK], BF16, name=f"result_bf{c}", align_bytes=64)
+            for u in range(2):
+                acc = psum.tile([P, 2, CHUNK], F32, name=f"acc{c}_{u}", tag=f"bank{2 * c + u}")
+                for e in range(2):
+                    t = 2 * u + e
+                    nc.tensor.matmul_mx(
+                        out=acc[:, e, :],
+                        lhsT=w2_codes[:, t * P : (t + 1) * P].bitcast(FP8X4),
+                        lhsT_scale=w2_scale[:, t * P : (t + 1) * P],
+                        rhs=z_codes[:, cols].bitcast(FP8X4),
+                        rhs_scale=z_scale[:, cols],
+                        start=True,
+                        stop=True,
+                    )
+                nc.scalar.copy(out=result[:, 2 * u : 2 * u + 2, :], in_=acc[:])
+                if c == 0:
+                    nc.sync.dma_start(out=out_rows[:, 2 * u : 2 * u + 2, cols], in_=result[:, 2 * u : 2 * u + 2, :])
+            if c > 0:
+                nc.sync.dma_start(out=out_rows[:, :, cols], in_=result[:])
             nc.vector.tensor_copy(
-                out=result_bf[:].rearrange("p (a i) t -> p a t i", i=4), in_=result[:].rearrange("p t (a i) -> p a t i", i=4)
+                out=result_bf[:, cols, :].rearrange("p (a i) t -> p a t i", i=4),
+                in_=result[:].rearrange("p t (a i) -> p a t i", i=4),
             )
-            nc.vector.quantize_mx(
-                out=out_codes[:, cols].bitcast(FP8X4), scales=out_scale[:, cols], in_=result_bf[:].rearrange("p n t -> p (n t)")
-            )
+            if c > 0:
+                span = slice(0 if c == 1 else c * CHUNK, (c + 1) * CHUNK)
+                nc.vector.quantize_mx(
+                    out=out_codes[:, span].bitcast(FP8X4),
+                    scales=out_scale[:, span],
+                    in_=result_bf[:, span, :].rearrange("p n t -> p (n t)"),
+                )
             if c % 2 == 1:
                 pair = slice((c - 1) * CHUNK, (c + 1) * CHUNK)
                 nc.sync.dma_start(out=out_words[:, pair], in_=out_codes[:, pair])

@@ -45,153 +45,203 @@ def tile_picked_deliver_gelu_po_kernel(
         x_table_scales = sb.tile([P, T], U8, name="x_table_scales", align_bytes=64)
         w2_raw = sb.tile([P, N], I32, name="w2_raw", tag="w2_raw", align_bytes=64)
         w2_raw_scales = sb.tile([P, N], U8, name="w2_raw_scales", tag="w2_raw_scales", align_bytes=64)
-        w1_raw = [sb.tile([P, PACK, H // 2], F32, name=f"w1_raw{u}", align_bytes=64) for u in range(2)]
         warm = sb.tile([P, 8], F32, name="warm")
         warm_out = sb.tile([P, 8], F32, name="warm_out")
 
         nc.vector.memset(x_table_scales[:].bitcast(I32), 0)
         nc.vector.memset(warm[:], 0.0)
         nc.gpsimd.memset(w2_raw_scales[:].bitcast(I32), 0)
-
-        w1_rows = w1.rearrange("(p j) c -> p j c", j=PACK)
         nc.scalar.activation(warm_out[:], warm[:], GELU)
-        nc.sync.dma_start(out=w1_raw[0][:], in_=w1_rows[:, :, 0 : H // 2])
+        w1_rows = w1.rearrange("(p j) c -> p j c", j=PACK)
+        w1_raw = sb.tile([P, PACK, H], F32, name="w1_raw", align_bytes=64)
+        nc.sync.dma_start(out=w1_raw[:, 0:2, :], in_=w1_rows[:, 0:2, :])
         load_scale_rows(nc.sync, x_table_scales, x_scales)
         nc.sync.dma_start(offs_sb[:], offs)
-        nc.sync.dma_start(out=w1_raw[1][:], in_=w1_rows[:, :, H // 2 : H])
+        nc.sync.dma_start(out=w1_raw[:, 2:4, :], in_=w1_rows[:, 2:4, :])
         nc.sync.dma_start(out=x_table[:], in_=as_words(x_words))
         nc.sync.dma_start(out=w2_raw[:], in_=as_words(w2_words))
         load_scale_rows(nc.sync, w2_raw_scales, w2_scales)
         nc.sync.dma_start(src_sb[:], src)
         nc.sync.dma_start(dst_sb[:], dst)
 
-        w1_bf = sb.tile([P, PACK, P, PACK], BF16, name="w1_bf", align_bytes=64)
+        order = [2, 3, 0, 1]
         x_scale = sb.tile([P, S], U8, name="x_scale", align_bytes=64)
-        for u in range(2):
+        nc.vector.tensor_copy(x_scale[:], x_table_scales[:].indirect(offs_sb[:]))
+        w1_bf = [sb.tile([P, 2, P, PACK], BF16, name=f"w1_bf{e}", tag=f"w1_bf{e}", align_bytes=64) for e in range(2)]
+        w1_codes = [sb.tile([P, 2 * P], U32, name=f"w1_codes{e}", align_bytes=64) for e in range(2)]
+        w1_scale = [sb.tile([P, 2 * P], U8, name=f"w1_scale{e}", align_bytes=64) for e in range(2)]
+        for e in (1, 0):
             nc.vector.tensor_copy(
-                out=w1_bf[:, :, u * 64 : (u + 1) * 64, :].rearrange("p t m j -> p m t j"),
-                in_=w1_raw[u][:].rearrange("p j (m t) -> p m t j", t=PACK),
+                out=w1_bf[e][:].rearrange("p t m j -> p m t j"),
+                in_=w1_raw[:].rearrange("p j (m t) -> p m t j", t=PACK)[:, :, 2 * e : 2 * e + 2, :],
             )
-            if u == 0:
-                nc.vector.tensor_copy(x_scale[:], x_table_scales[:].indirect(offs_sb[:]))
-        w1_codes = sb.tile([P, H], U32, name="w1_codes", align_bytes=64)
-        w1_scale = sb.tile([P, H], U8, name="w1_scale", align_bytes=64)
-        nc.vector.quantize_mx(out=w1_codes[:].bitcast(FP8X4), scales=w1_scale[:], in_=w1_bf[:].rearrange("p t m j -> p (t m j)"))
-
-        x_codes = [sb.tile([P, HALF], U32, name=f"x_codes{h}", align_bytes=64) for h in range(2)]
+        for e in (1, 0):
+            nc.vector.quantize_mx(out=w1_codes[e][:].bitcast(FP8X4), scales=w1_scale[e][:], in_=w1_bf[e][:].rearrange("p t m j -> p (t m j)"))
+        x_codes = [sb.tile([P, HALF], U32, name=f"x_codes{h}", tag=f"x_codes{h}", align_bytes=64) for h in range(2)]
         for h in range(2):
             nc.vector.tensor_copy(x_codes[h][:], x_table[:].bitcast(U32).indirect(offs_sb[:, h * 16 : (h + 1) * 16]))
 
-        order = [2, 0, 1, 3]
         z = [sb.tile([P, S], F32, name=f"z{t}", tag=f"z{t}", align_bytes=64) for t in range(PACK)]
 
-        def first_product(acc, t, h):
+        def first_product(acc, t, start, width):
+            h, at = divmod(start, HALF)
             nc.tensor.matmul_mx(
                 out=acc,
-                lhsT=w1_codes[:, t * P : (t + 1) * P].bitcast(FP8X4),
-                lhsT_scale=w1_scale[:, t * P : (t + 1) * P],
-                rhs=x_codes[h][:].bitcast(FP8X4),
-                rhs_scale=x_scale[:, h * HALF : (h + 1) * HALF],
+                lhsT=w1_codes[t // 2][:, t % 2 * P : (t % 2 + 1) * P].bitcast(FP8X4),
+                lhsT_scale=w1_scale[t // 2][:, t % 2 * P : (t % 2 + 1) * P],
+                rhs=x_codes[h][:, at : at + width].bitcast(FP8X4),
+                rhs_scale=x_scale[:, start : start + width],
                 start=True,
                 stop=True,
             )
 
-        lead = [psum.tile([P, HALF], F32, name=f"lead{h}", tag=f"bank{h}") for h in range(2)]
-        rest = [psum.tile([P, S], F32, name=f"rest{i}", tag=f"bank{2 + i}") for i in range(3)]
-        first_product(lead[0][:], order[0], 0)
-        first_product(rest[0][:, 0:HALF], order[1], 0)
-        first_product(lead[1][:], order[0], 1)
-        first_product(rest[0][:, HALF:S], order[1], 1)
+        lead_parts = [(0, HALF), (HALF, HALF)]
+        lead = [psum.tile([P, width], F32, name=f"lead{i}", tag=f"bank{i}") for i, (start, width) in enumerate(lead_parts)]
+        rest = [psum.tile([P, S], F32, name=f"rest{i}", tag=f"bank{3 + i}") for i in range(3)]
+        first_product(lead[0][:], order[0], 0, HALF)
+        first_product(rest[0][:, 0:HALF], order[1], 0, HALF)
+        for i in range(1, len(lead_parts)):
+            first_product(lead[i][:], order[0], *lead_parts[i])
+        first_product(rest[0][:, HALF:S], order[1], HALF, HALF)
         for i in (1, 2):
             for h in range(2):
-                first_product(rest[i][:, h * HALF : (h + 1) * HALF], order[i + 1], h)
-        for h in range(2):
-            nc.scalar.copy(out=z[order[0]][:, h * HALF : (h + 1) * HALF], in_=lead[h][:])
-        for i in range(3):
-            nc.scalar.copy(out=z[order[i + 1]][:], in_=rest[i][:])
+                first_product(rest[i][:, h * HALF : (h + 1) * HALF], order[i + 1], h * HALF, HALF)
+        for i, (start, width) in enumerate(lead_parts):
+            if i == 2:
+                nc.vector.tensor_copy(out=z[order[0]][:, start : start + width], in_=lead[i][:])
+            else:
+                nc.scalar.copy(out=z[order[0]][:, start : start + width], in_=lead[i][:])
 
         w2_codes = sb.tile([P, N], I32, name="w2_codes", align_bytes=64)
-        w2_scale = sb.tile([P, N], U8, name="w2_scale", align_bytes=64)
+        w2_scale = [sb.tile([P, 3 * P], U8, name="w2_scale_early", align_bytes=64)]
         nc.vector.tensor_copy(
             out=w2_codes[:].rearrange("p (t m) -> p m t", t=PACK), in_=w2_raw[:].rearrange("p (m t) -> p m t", t=PACK)
         )
         nc.vector.tensor_copy(
-            out=w2_scale[:].rearrange("p (t m) -> p m t", t=PACK), in_=w2_raw_scales[:].rearrange("p (m t) -> p m t", t=PACK)
+            out=w2_scale[0][:].rearrange("p (t m) -> p m t", t=3), in_=w2_raw_scales[:].rearrange("p (m t) -> p m t", t=PACK)[:, :, 0:3]
         )
-
-        fetched = [
-            sb.tile([P, V], F32, name=f"fetched{t}", tag={order[0]: "w2_raw", order[1]: "w2_raw_scales"}.get(t, f"fetched{t}"), align_bytes=64)
-            for t in range(PACK)
-        ]
+        fetched = [sb.tile([P, V], F32, name=f"fetched{t}", tag={order[0]: "w2_raw", order[1]: "fetched_b"}.get(t, f"fetched{t}"), align_bytes=64) for t in range(PACK)]
         last = order[3]
-        for t in order:
-            nc.vector.tensor_copy(fetched[t][:], z[t][:].indirect(src_sb[:]))
-        message = {t: sb.tile([P, V], F32, name=f"message{t}", align_bytes=64) for t in order}
-        for t in order:
-            nc.scalar.activation(message[t][:], fetched[t][:], GELU)
+        message = {t: sb.tile([P, V], F32, name=f"message{t}", tag=f"message{t}", align_bytes=64) for t in order}
         z_bf = sb.tile([P, S, PACK], BF16, name="z_bf", align_bytes=64)
-        for t in order:
-            nc.vector.tensor_copy(z[t][:].indirect(dst_sb[:]), message[t][:])
-        nc.scalar.copy(out=z_bf[:, 0:CHUNK, 2:4], in_=z[order[0]][:, 0:CHUNK].rearrange("p (n o) -> p n o", o=1).to_broadcast([P, CHUNK, 2]))
-        nc.scalar.copy(out=z_bf[:, CHUNK:S, order[0]], in_=z[order[0]][:, CHUNK:S])
-        nc.scalar.copy(out=z_bf[:, :, order[1]], in_=z[order[1]][:])
+
+        def evict(i):
+            nc.scalar.copy(out=z[order[i]][:], in_=rest[i - 1][:])
+
+        def fetch(i):
+            nc.vector.tensor_copy(fetched[order[i]][:], z[order[i]][:].indirect(src_sb[:]))
+
+        def activate(i):
+            nc.scalar.activation(message[order[i]][:], fetched[order[i]][:], GELU)
+
+        def deliver(i):
+            nc.vector.tensor_copy(z[order[i]][:].indirect(dst_sb[:]), message[order[i]][:])
+
+        for i in (1, 2, 3):
+            evict(i)
+        for step in (fetch, activate):
+            for i in range(PACK):
+                step(i)
+        deliver(0)
+        deliver(1)
+        w2_scale.append(sb.tile([P, P], U8, name="w2_scale_late", tag=f"message{order[1]}", align_bytes=64))
+        nc.vector.tensor_copy(out=w2_scale[1][:], in_=w2_raw_scales[:].rearrange("p (m t) -> p m t", t=PACK)[:, :, 3])
         for h in range(2):
-            nc.scalar.copy(out=z_bf[:, h * HALF : (h + 1) * HALF, order[2]], in_=z[order[2]][:, h * HALF : (h + 1) * HALF])
+            idle = psum.tile([P, S], F32, name=f"idle{h}", tag=f"bank{6 + h}")
+            nc.tensor.matmul_mx(
+                out=idle[:],
+                lhsT=w2_codes[:, 3 * P : 4 * P].bitcast(FP8X4),
+                lhsT_scale=w2_scale[1][:],
+                rhs=w2_codes[:].bitcast(FP8X4),
+                rhs_scale=w2_raw_scales[:],
+                start=True,
+                stop=True,
+            )
+        deliver(2)
+        deliver(3)
+        nc.scalar.copy(out=z_bf[:, :, order[0]], in_=z[order[0]][:])
+        nc.scalar.copy(out=z_bf[:, :, order[1]], in_=z[order[1]][:])
+        nc.scalar.copy(out=z_bf[:, 0:HALF, 0:2], in_=z[order[2]][:, 0:HALF].rearrange("p (n o) -> p n o", o=1).to_broadcast([P, HALF, 2]))
+        nc.scalar.copy(out=z_bf[:, HALF:S, order[2]], in_=z[order[2]][:, HALF:S])
+        chunk = [slice(c * CHUNK, (c + 1) * CHUNK) for c in range(CHUNKS)]
         for c in range(CHUNKS):
-            cols = slice(c * CHUNK, (c + 1) * CHUNK)
-            if c == 0:
-                nc.vector.tensor_copy(out=z_bf[:, cols, last], in_=z[last][:, cols])
+            if c < 2:
+                nc.vector.tensor_copy(out=z_bf[:, chunk[c], last], in_=z[last][:, chunk[c]])
             else:
-                nc.scalar.copy(out=z_bf[:, cols, last], in_=z[last][:, cols])
+                nc.scalar.copy(out=z_bf[:, chunk[c], last], in_=z[last][:, chunk[c]])
 
         z_codes = sb.tile([P, S], U32, name="z_codes", align_bytes=64)
         z_scale = sb.tile([P, S], U8, name="z_scale", align_bytes=64)
         for c in range(CHUNKS):
-            cols = slice(c * CHUNK, (c + 1) * CHUNK)
             nc.vector.quantize_mx(
-                out=z_codes[:, cols].bitcast(FP8X4), scales=z_scale[:, cols], in_=z_bf[:, cols, :].rearrange("p n t -> p (n t)")
+                out=z_codes[:, chunk[c]].bitcast(FP8X4), scales=z_scale[:, chunk[c]], in_=z_bf[:, chunk[c], :].rearrange("p n t -> p (n t)")
             )
 
         out_rows = out_0.rearrange("(p t) n -> p t n", t=PACK)
         out_words = as_words(out_1)
         out_codes = sb.tile([P, S], I32, name="out_codes", align_bytes=64)
         out_scale = sb.tile([P, S], U8, name="out_scale", align_bytes=64)
-        result_bf = sb.tile([P, S, PACK], BF16, name="result_bf", align_bytes=64)
-        for c in range(CHUNKS):
-            cols = slice(c * CHUNK, (c + 1) * CHUNK)
-            result = sb.tile([P, PACK, CHUNK], F32, name=f"result{c}", align_bytes=64)
-            for u in range(2):
-                acc = psum.tile([P, 2, CHUNK], F32, name=f"acc{c}_{u}", tag=f"bank{2 * c + u}")
-                for e in range(2):
-                    t = 2 * u + e
-                    nc.tensor.matmul_mx(
-                        out=acc[:, e, :],
-                        lhsT=w2_codes[:, t * P : (t + 1) * P].bitcast(FP8X4),
-                        lhsT_scale=w2_scale[:, t * P : (t + 1) * P],
-                        rhs=z_codes[:, cols].bitcast(FP8X4),
-                        rhs_scale=z_scale[:, cols],
-                        start=True,
-                        stop=True,
-                    )
-                nc.scalar.copy(out=result[:, 2 * u : 2 * u + 2, :], in_=acc[:])
-                if c == 0:
-                    nc.sync.dma_start(out=out_rows[:, 2 * u : 2 * u + 2, cols], in_=result[:, 2 * u : 2 * u + 2, :])
-            if c > 0:
-                nc.sync.dma_start(out=out_rows[:, :, cols], in_=result[:])
-            nc.vector.tensor_copy(
-                out=result_bf[:, cols, :].rearrange("p (a i) t -> p a t i", i=4),
-                in_=result[:].rearrange("p t (a i) -> p a t i", i=4),
-            )
-            if c > 0:
-                span = slice(0 if c == 1 else c * CHUNK, (c + 1) * CHUNK)
-                nc.vector.quantize_mx(
-                    out=out_codes[:, span].bitcast(FP8X4),
-                    scales=out_scale[:, span],
-                    in_=result_bf[:, span, :].rearrange("p n t -> p (n t)"),
+        result = [sb.tile([P, PACK, CHUNK], F32, name=f"result{c}", align_bytes=64) for c in range(CHUNKS)]
+        result_bf = [sb.tile([P, HALF, PACK], BF16, name=f"result_bf{h}", align_bytes=64) for h in range(2)]
+
+        def rounded(c):
+            return result_bf[c // 2][:, c % 2 * CHUNK : (c % 2 + 1) * CHUNK, :]
+
+        def second_product(c, planes, bank):
+            acc = psum.tile([P, len(planes), CHUNK], F32, name=f"acc{bank}", tag=f"bank{bank}")
+            for e, t in enumerate(planes):
+                nc.tensor.matmul_mx(
+                    out=acc[:, e, :],
+                    lhsT=w2_codes[:, t * P : (t + 1) * P].bitcast(FP8X4),
+                    lhsT_scale=w2_scale[t // 3][:, t % 3 * P : (t % 3 + 1) * P],
+                    rhs=z_codes[:, chunk[c]].bitcast(FP8X4),
+                    rhs_scale=z_scale[:, chunk[c]],
+                    start=True,
+                    stop=True,
                 )
-            if c % 2 == 1:
-                pair = slice((c - 1) * CHUNK, (c + 1) * CHUNK)
-                nc.sync.dma_start(out=out_words[:, pair], in_=out_codes[:, pair])
+            return acc
+
+        def empty(copy, acc, c, planes):
+            rows = slice(planes[0], planes[-1] + 1)
+            copy(out=result[c][:, rows, :], in_=acc[:])
+            nc.sync.dma_start(out=out_rows[:, rows, chunk[c]], in_=result[c][:, rows, :])
+
+        def interleave(c):
+            nc.vector.tensor_copy(
+                out=rounded(c).rearrange("p (a i) t -> p a t i", i=4),
+                in_=result[c][:].rearrange("p t (a i) -> p a t i", i=4),
+            )
+
+        def interleave_bank(copy, acc, c):
+            copy(out=rounded(c), in_=acc[:].rearrange("p t n -> p n t"))
+
+        def quantise_out(c, count):
+            span = slice(c * CHUNK, (c + count) * CHUNK)
+            at = c % 2 * CHUNK
+            nc.vector.quantize_mx(
+                out=out_codes[:, span].bitcast(FP8X4),
+                scales=out_scale[:, span],
+                in_=result_bf[c // 2][:, at : at + count * CHUNK, :].rearrange("p n t -> p (n t)"),
+            )
+
+        def store_words(queue, c, count):
+            span = slice(c * CHUNK, (c + count) * CHUNK)
+            queue.dma_start(out=out_words[:, span], in_=out_codes[:, span])
+
+        every = range(PACK)
+        empty(nc.scalar.copy, second_product(0, (0, 1), 0), 0, (0, 1))
+        empty(nc.scalar.copy, second_product(0, (2, 3), 1), 0, (2, 3))
+        empty(nc.vector.tensor_copy, second_product(1, every, 2), 1, every)
+        empty(nc.scalar.copy, second_product(2, every, 3), 2, every)
+        final = second_product(3, every, 4)
+        empty(nc.scalar.copy, final, 3, every)
+        interleave_bank(nc.scalar.copy, final, 3)
+        for c in range(3):
+            interleave(c)
+        quantise_out(0, 2)
+        store_words(nc.sync, 0, 2)
+        quantise_out(2, 2)
+        store_words(nc.sync, 2, 2)
         for q in range(4):
             queue = nc.scalar if q % 2 else nc.sync
             queue.dma_start(out=out_2[0, 4 * q : 4 * q + 4, :].bitcast(I32), in_=out_scale[32 * q : 32 * q + 4, :].bitcast(I32))

@@ -53,11 +53,11 @@ def tile_picked_deliver_gelu_po_kernel(
         nc.gpsimd.memset(w2_raw_scales[:].bitcast(I32), 0)
         nc.scalar.activation(warm_out[:], warm[:], GELU)
         w1_rows = w1.rearrange("(p j) c -> p j c", j=PACK)
-        w1_raw = sb.tile([P, PACK, H], F32, name="w1_raw", align_bytes=64)
-        nc.sync.dma_start(out=w1_raw[:, 0:2, :], in_=w1_rows[:, 0:2, :])
+        w1_raw = [sb.tile([P, PACK, H // 2], F32, name=f"w1_raw{u}", align_bytes=64) for u in range(2)]
+        nc.sync.dma_start(out=w1_raw[0][:], in_=w1_rows[:, :, 0 : H // 2])
         load_scale_rows(nc.sync, x_table_scales, x_scales)
         nc.sync.dma_start(offs_sb[:], offs)
-        nc.sync.dma_start(out=w1_raw[:, 2:4, :], in_=w1_rows[:, 2:4, :])
+        nc.sync.dma_start(out=w1_raw[1][:], in_=w1_rows[:, :, H // 2 : H])
         nc.sync.dma_start(out=x_table[:], in_=as_words(x_words))
         nc.sync.dma_start(out=w2_raw[:], in_=as_words(w2_words))
         load_scale_rows(nc.sync, w2_raw_scales, w2_scales)
@@ -65,18 +65,18 @@ def tile_picked_deliver_gelu_po_kernel(
         nc.sync.dma_start(dst_sb[:], dst)
 
         order = [2, 3, 0, 1]
+        w1_bf = sb.tile([P, PACK, P, PACK], BF16, name="w1_bf", align_bytes=64)
         x_scale = sb.tile([P, S], U8, name="x_scale", align_bytes=64)
-        nc.vector.tensor_copy(x_scale[:], x_table_scales[:].indirect(offs_sb[:]))
-        w1_bf = [sb.tile([P, 2, P, PACK], BF16, name=f"w1_bf{e}", tag=f"w1_bf{e}", align_bytes=64) for e in range(2)]
-        w1_codes = [sb.tile([P, 2 * P], U32, name=f"w1_codes{e}", align_bytes=64) for e in range(2)]
-        w1_scale = [sb.tile([P, 2 * P], U8, name=f"w1_scale{e}", align_bytes=64) for e in range(2)]
-        for e in (1, 0):
+        for u in range(2):
             nc.vector.tensor_copy(
-                out=w1_bf[e][:].rearrange("p t m j -> p m t j"),
-                in_=w1_raw[:].rearrange("p j (m t) -> p m t j", t=PACK)[:, :, 2 * e : 2 * e + 2, :],
+                out=w1_bf[:, :, u * 64 : (u + 1) * 64, :].rearrange("p t m j -> p m t j"),
+                in_=w1_raw[u][:].rearrange("p j (m t) -> p m t j", t=PACK),
             )
-        for e in (1, 0):
-            nc.vector.quantize_mx(out=w1_codes[e][:].bitcast(FP8X4), scales=w1_scale[e][:], in_=w1_bf[e][:].rearrange("p t m j -> p (t m j)"))
+            if u == 0:
+                nc.vector.tensor_copy(x_scale[:], x_table_scales[:].indirect(offs_sb[:]))
+        w1_codes = sb.tile([P, H], U32, name="w1_codes", align_bytes=64)
+        w1_scale = sb.tile([P, H], U8, name="w1_scale", align_bytes=64)
+        nc.vector.quantize_mx(out=w1_codes[:].bitcast(FP8X4), scales=w1_scale[:], in_=w1_bf[:].rearrange("p t m j -> p (t m j)"))
         x_codes = [sb.tile([P, HALF], U32, name=f"x_codes{h}", tag=f"x_codes{h}", align_bytes=64) for h in range(2)]
         for h in range(2):
             nc.vector.tensor_copy(x_codes[h][:], x_table[:].bitcast(U32).indirect(offs_sb[:, h * 16 : (h + 1) * 16]))
@@ -87,8 +87,8 @@ def tile_picked_deliver_gelu_po_kernel(
             h, at = divmod(start, HALF)
             nc.tensor.matmul_mx(
                 out=acc,
-                lhsT=w1_codes[t // 2][:, t % 2 * P : (t % 2 + 1) * P].bitcast(FP8X4),
-                lhsT_scale=w1_scale[t // 2][:, t % 2 * P : (t % 2 + 1) * P],
+                lhsT=w1_codes[:, t * P : (t + 1) * P].bitcast(FP8X4),
+                lhsT_scale=w1_scale[:, t * P : (t + 1) * P],
                 rhs=x_codes[h][:, at : at + width].bitcast(FP8X4),
                 rhs_scale=x_scale[:, start : start + width],
                 start=True,
@@ -144,8 +144,9 @@ def tile_picked_deliver_gelu_po_kernel(
                 step(i)
         deliver(0)
         deliver(1)
-        w2_scale.append(sb.tile([P, P], U8, name="w2_scale_late", tag=f"message{order[1]}", align_bytes=64))
-        nc.vector.tensor_copy(out=w2_scale[1][:], in_=w2_raw_scales[:].rearrange("p (m t) -> p m t", t=PACK)[:, :, 3])
+        deliver(2)
+        w2_scale.append(sb.tile([P, P], U8, name="w2_scale_late", tag=f"message{order[2]}", align_bytes=64))
+        nc.gpsimd.tensor_copy(out=w2_scale[1][:], in_=w2_raw_scales[:].rearrange("p (m t) -> p m t", t=PACK)[:, :, 3])
         for h in range(2):
             idle = psum.tile([P, S], F32, name=f"idle{h}", tag=f"bank{6 + h}")
             nc.tensor.matmul_mx(
@@ -157,7 +158,6 @@ def tile_picked_deliver_gelu_po_kernel(
                 start=True,
                 stop=True,
             )
-        deliver(2)
         deliver(3)
         nc.scalar.copy(out=z_bf[:, :, order[0]], in_=z[order[0]][:])
         nc.scalar.copy(out=z_bf[:, :, order[1]], in_=z[order[1]][:])
@@ -230,17 +230,19 @@ def tile_picked_deliver_gelu_po_kernel(
 
         every = range(PACK)
         empty(nc.scalar.copy, second_product(0, (0, 1), 0), 0, (0, 1))
-        empty(nc.scalar.copy, second_product(0, (2, 3), 1), 0, (2, 3))
-        empty(nc.vector.tensor_copy, second_product(1, every, 2), 1, every)
-        empty(nc.scalar.copy, second_product(2, every, 3), 2, every)
-        final = second_product(3, every, 4)
+        empty(nc.vector.tensor_copy, second_product(0, (2, 3), 1), 0, (2, 3))
+        empty(nc.scalar.copy, second_product(1, (0, 1), 2), 1, (0, 1))
+        empty(nc.vector.tensor_copy, second_product(1, (2, 3), 3), 1, (2, 3))
+        empty(nc.scalar.copy, second_product(2, every, 4), 2, every)
+        final = second_product(3, every, 5)
         empty(nc.scalar.copy, final, 3, every)
         interleave_bank(nc.scalar.copy, final, 3)
         for c in range(3):
             interleave(c)
         quantise_out(0, 2)
         store_words(nc.sync, 0, 2)
-        quantise_out(2, 2)
+        quantise_out(2, 1)
+        quantise_out(3, 1)
         store_words(nc.sync, 2, 2)
         for q in range(4):
             queue = nc.scalar if q % 2 else nc.sync

@@ -16,18 +16,22 @@ GELU = mybir.ActivationFunctionType.Gelu_apprx_tanh
 
 P = 128
 PACK = 4
+LIST_ROWS = 16
 HALF = S // 2
 CHUNK = 128
 CHUNKS = S // CHUNK
+ORDER = (2, 3, 0, 1)
+BANKS_ON_VECTOR = ((0, 1), (2, 1))
+CHUNK_ON_SCALAR = 2
 
 
 def as_words(packed):
     return packed[0].rearrange("p n t -> p (n t)").bitcast(I32)
 
 
-def load_scale_rows(queue, plane, scales):
+def load_scale_rows(queue, tile, scales):
     for q in range(4):
-        queue.dma_start(out=plane[32 * q : 32 * q + 4, :].bitcast(I32), in_=scales[0, 4 * q : 4 * q + 4, :].bitcast(I32))
+        queue.dma_start(out=tile[32 * q : 32 * q + 4, :].bitcast(I32), in_=scales[0, 4 * q : 4 * q + 4, :].bitcast(I32))
 
 
 def tile_picked_deliver_gelu_po_kernel(
@@ -38,20 +42,17 @@ def tile_picked_deliver_gelu_po_kernel(
         sb = ctx.enter_context(tc.tile_pool(name="sb", bufs=1))
         psum = ctx.enter_context(tc.psum_pool(name="psum", bufs=1))
 
-        offs_sb = sb.tile([P, S // 16], U16, name="offs_sb")
-        src_sb = sb.tile([P, V // 16], U16, name="src_sb")
-        dst_sb = sb.tile([P, V // 16], U16, name="dst_sb")
+        offs_sb = sb.tile([P, S // LIST_ROWS], U16, name="offs_sb")
+        src_sb = sb.tile([P, V // LIST_ROWS], U16, name="src_sb")
+        dst_sb = sb.tile([P, V // LIST_ROWS], U16, name="dst_sb")
         x_table = sb.tile([P, T], I32, name="x_table", align_bytes=64)
         x_table_scales = sb.tile([P, T], U8, name="x_table_scales", align_bytes=64)
         w2_raw = sb.tile([P, N], I32, name="w2_raw", tag="w2_raw", align_bytes=64)
         w2_raw_scales = sb.tile([P, N], U8, name="w2_raw_scales", tag="w2_raw_scales", align_bytes=64)
-        warm = sb.tile([P, 8], F32, name="warm")
-        warm_out = sb.tile([P, 8], F32, name="warm_out")
 
         nc.vector.memset(x_table_scales[:].bitcast(I32), 0)
-        nc.vector.memset(warm[:], 0.0)
         nc.gpsimd.memset(w2_raw_scales[:].bitcast(I32), 0)
-        nc.scalar.activation(warm_out[:], warm[:], GELU)
+
         w1_rows = w1.rearrange("(p j) c -> p j c", j=PACK)
         w1_raw = [sb.tile([P, PACK, H // 2], F32, name=f"w1_raw{u}", align_bytes=64) for u in range(2)]
         nc.sync.dma_start(out=w1_raw[0][:], in_=w1_rows[:, :, 0 : H // 2])
@@ -64,12 +65,11 @@ def tile_picked_deliver_gelu_po_kernel(
         nc.sync.dma_start(src_sb[:], src)
         nc.sync.dma_start(dst_sb[:], dst)
 
-        order = [2, 3, 0, 1]
         w1_bf = sb.tile([P, PACK, P, PACK], BF16, name="w1_bf", align_bytes=64)
         x_scale = sb.tile([P, S], U8, name="x_scale", align_bytes=64)
         for u in range(2):
             nc.vector.tensor_copy(
-                out=w1_bf[:, :, u * 64 : (u + 1) * 64, :].rearrange("p t m j -> p m t j"),
+                out=w1_bf[:, :, u * P // 2 : (u + 1) * P // 2, :].rearrange("p t m j -> p m t j"),
                 in_=w1_raw[u][:].rearrange("p j (m t) -> p m t j", t=PACK),
             )
             if u == 0:
@@ -77,98 +77,88 @@ def tile_picked_deliver_gelu_po_kernel(
         w1_codes = sb.tile([P, H], U32, name="w1_codes", align_bytes=64)
         w1_scale = sb.tile([P, H], U8, name="w1_scale", align_bytes=64)
         nc.vector.quantize_mx(out=w1_codes[:].bitcast(FP8X4), scales=w1_scale[:], in_=w1_bf[:].rearrange("p t m j -> p (t m j)"))
-        x_codes = [sb.tile([P, HALF], U32, name=f"x_codes{h}", tag=f"x_codes{h}", align_bytes=64) for h in range(2)]
+
+        columns = HALF // LIST_ROWS
+        x_codes = [sb.tile([P, HALF], U32, name=f"x_codes{h}", align_bytes=64) for h in range(2)]
         for h in range(2):
-            nc.vector.tensor_copy(x_codes[h][:], x_table[:].bitcast(U32).indirect(offs_sb[:, h * 16 : (h + 1) * 16]))
+            nc.vector.tensor_copy(x_codes[h][:], x_table[:].bitcast(U32).indirect(offs_sb[:, h * columns : (h + 1) * columns]))
 
-        z = [sb.tile([P, S], F32, name=f"z{t}", tag=f"z{t}", align_bytes=64) for t in range(PACK)]
-
-        def first_product(acc, t, start, width):
-            h, at = divmod(start, HALF)
+        def first_product(acc, t, tokens):
+            h, at = divmod(tokens.start, HALF)
             nc.tensor.matmul_mx(
                 out=acc,
                 lhsT=w1_codes[:, t * P : (t + 1) * P].bitcast(FP8X4),
                 lhsT_scale=w1_scale[:, t * P : (t + 1) * P],
-                rhs=x_codes[h][:, at : at + width].bitcast(FP8X4),
-                rhs_scale=x_scale[:, start : start + width],
+                rhs=x_codes[h][:, at : at + tokens.stop - tokens.start].bitcast(FP8X4),
+                rhs_scale=x_scale[:, tokens],
                 start=True,
                 stop=True,
             )
 
-        lead_parts = [(0, HALF), (HALF, HALF)]
-        lead = [psum.tile([P, width], F32, name=f"lead{i}", tag=f"bank{i}") for i, (start, width) in enumerate(lead_parts)]
-        rest = [psum.tile([P, S], F32, name=f"rest{i}", tag=f"bank{3 + i}") for i in range(3)]
-        first_product(lead[0][:], order[0], 0, HALF)
-        first_product(rest[0][:, 0:HALF], order[1], 0, HALF)
-        for i in range(1, len(lead_parts)):
-            first_product(lead[i][:], order[0], *lead_parts[i])
-        first_product(rest[0][:, HALF:S], order[1], HALF, HALF)
-        for i in (1, 2):
-            for h in range(2):
-                first_product(rest[i][:, h * HALF : (h + 1) * HALF], order[i + 1], h * HALF, HALF)
-        for i, (start, width) in enumerate(lead_parts):
-            if i == 2:
-                nc.vector.tensor_copy(out=z[order[0]][:, start : start + width], in_=lead[i][:])
-            else:
-                nc.scalar.copy(out=z[order[0]][:, start : start + width], in_=lead[i][:])
+        first, second, third, last = ORDER
+        halves = [slice(h * HALF, (h + 1) * HALF) for h in range(2)]
+        chunk = [slice(c * CHUNK, (c + 1) * CHUNK) for c in range(CHUNKS)]
+        first_parts = [halves[0], chunk[2], chunk[3]]
+        first_banks = [psum.tile([P, part.stop - part.start], F32, name=f"y_first{i}", tag=f"bank{i}") for i, part in enumerate(first_parts)]
+        y_bank = {t: psum.tile([P, S], F32, name=f"y{t}", tag=f"bank{len(first_parts) + i}") for i, t in enumerate(ORDER[1:])}
+        first_product(first_banks[0][:], first, first_parts[0])
+        first_product(y_bank[second][:, halves[0]], second, halves[0])
+        for bank, part in zip(first_banks[1:], first_parts[1:]):
+            first_product(bank[:], first, part)
+        first_product(y_bank[second][:, halves[1]], second, halves[1])
+        for t in (third, last):
+            for half in halves:
+                first_product(y_bank[t][:, half], t, half)
+
+        first_gelu = sb.tile([P, S], F32, name="first_gelu", align_bytes=64)
+        for bank, part in zip(first_banks, first_parts):
+            nc.scalar.activation(first_gelu[:, part], bank[:], GELU)
 
         w2_codes = sb.tile([P, N], I32, name="w2_codes", align_bytes=64)
-        w2_scale = [sb.tile([P, 3 * P], U8, name="w2_scale_early", align_bytes=64)]
-        nc.vector.tensor_copy(
-            out=w2_codes[:].rearrange("p (t m) -> p m t", t=PACK), in_=w2_raw[:].rearrange("p (m t) -> p m t", t=PACK)
-        )
-        nc.vector.tensor_copy(
-            out=w2_scale[0][:].rearrange("p (t m) -> p m t", t=3), in_=w2_raw_scales[:].rearrange("p (m t) -> p m t", t=PACK)[:, :, 0:3]
-        )
-        fetched = [sb.tile([P, V], F32, name=f"fetched{t}", tag={order[0]: "w2_raw", order[1]: "fetched_b"}.get(t, f"fetched{t}"), align_bytes=64) for t in range(PACK)]
-        last = order[3]
-        message = {t: sb.tile([P, V], F32, name=f"message{t}", tag=f"message{t}", align_bytes=64) for t in order}
+        w2_scale = sb.tile([P, N], U8, name="w2_scale", align_bytes=64)
+        for dealt, raw in ((w2_codes, w2_raw), (w2_scale, w2_raw_scales)):
+            nc.vector.tensor_copy(out=dealt[:].rearrange("p (t m) -> p m t", t=PACK), in_=raw[:].rearrange("p (m t) -> p m t", t=PACK))
+
+        z = [sb.tile([P, S], F32, name=f"z{t}", tag="w2_raw_scales" if t == first else f"z{t}", align_bytes=64) for t in range(PACK)]
+        fetched = [sb.tile([P, V], F32, name=f"fetched{t}", tag="w2_raw" if t == first else f"fetched{t}", align_bytes=64) for t in range(PACK)]
+        message = {t: sb.tile([P, V], F32, name=f"message{t}", align_bytes=64) for t in ORDER[1:]}
+        message[first] = fetched[first]
         z_bf = sb.tile([P, S, PACK], BF16, name="z_bf", align_bytes=64)
 
-        def evict(i):
-            nc.scalar.copy(out=z[order[i]][:], in_=rest[i - 1][:])
+        def fetch(t, window):
+            nc.vector.tensor_copy(fetched[t][:], window[:].indirect(src_sb[:]))
 
-        def fetch(i):
-            nc.vector.tensor_copy(fetched[order[i]][:], z[order[i]][:].indirect(src_sb[:]))
+        def activate(t):
+            nc.scalar.activation(message[t][:], fetched[t][:], GELU)
 
-        def activate(i):
-            nc.scalar.activation(message[order[i]][:], fetched[order[i]][:], GELU)
+        def deliver(t):
+            nc.vector.tensor_copy(z[t][:].indirect(dst_sb[:]), message[t][:])
 
-        def deliver(i):
-            nc.vector.tensor_copy(z[order[i]][:].indirect(dst_sb[:]), message[order[i]][:])
+        nc.scalar.copy(out=z[second][:], in_=y_bank[second][:])
+        for bank, part in zip(first_banks, first_parts):
+            nc.scalar.copy(out=z[first][:, part], in_=bank[:])
+        for t in (third, last):
+            nc.scalar.copy(out=z[t][:], in_=y_bank[t][:])
 
-        for i in (1, 2, 3):
-            evict(i)
-        for step in (fetch, activate):
-            for i in range(PACK):
-                step(i)
-        deliver(0)
-        deliver(1)
-        deliver(2)
-        w2_scale.append(sb.tile([P, P], U8, name="w2_scale_late", tag=f"message{order[2]}", align_bytes=64))
-        nc.gpsimd.tensor_copy(out=w2_scale[1][:], in_=w2_raw_scales[:].rearrange("p (m t) -> p m t", t=PACK)[:, :, 3])
-        for h in range(2):
-            idle = psum.tile([P, S], F32, name=f"idle{h}", tag=f"bank{6 + h}")
-            nc.tensor.matmul_mx(
-                out=idle[:],
-                lhsT=w2_codes[:, 3 * P : 4 * P].bitcast(FP8X4),
-                lhsT_scale=w2_scale[1][:],
-                rhs=w2_codes[:].bitcast(FP8X4),
-                rhs_scale=w2_raw_scales[:],
-                start=True,
-                stop=True,
-            )
-        deliver(3)
-        nc.scalar.copy(out=z_bf[:, :, order[0]], in_=z[order[0]][:])
-        nc.scalar.copy(out=z_bf[:, :, order[1]], in_=z[order[1]][:])
-        nc.scalar.copy(out=z_bf[:, 0:HALF, 0:2], in_=z[order[2]][:, 0:HALF].rearrange("p (n o) -> p n o", o=1).to_broadcast([P, HALF, 2]))
-        nc.scalar.copy(out=z_bf[:, HALF:S, order[2]], in_=z[order[2]][:, HALF:S])
-        chunk = [slice(c * CHUNK, (c + 1) * CHUNK) for c in range(CHUNKS)]
+        fetch(first, first_gelu)
+        fetch(second, z[second])
+        deliver(first)
+        fetch(third, z[third])
+        fetch(last, z[last])
+        for step in (activate, deliver):
+            for t in ORDER[1:]:
+                step(t)
+        for t in (first, second):
+            nc.scalar.copy(out=z_bf[:, :, t], in_=z[t][:])
+
+        nc.scalar.copy(
+            out=z_bf[:, halves[0], third : last + 1],
+            in_=z[third][:, halves[0]].rearrange("p (n o) -> p n o", o=1).to_broadcast([P, HALF, 2]),
+        )
+        nc.scalar.copy(out=z_bf[:, halves[1], third], in_=z[third][:, halves[1]])
         for c in range(CHUNKS):
-            if c < 2:
-                nc.vector.tensor_copy(out=z_bf[:, chunk[c], last], in_=z[last][:, chunk[c]])
-            else:
-                nc.scalar.copy(out=z_bf[:, chunk[c], last], in_=z[last][:, chunk[c]])
+            copy = nc.vector.tensor_copy if c < CHUNKS // 2 else nc.scalar.copy
+            copy(out=z_bf[:, chunk[c], last], in_=z[last][:, chunk[c]])
 
         z_codes = sb.tile([P, S], U32, name="z_codes", align_bytes=64)
         z_scale = sb.tile([P, S], U8, name="z_scale", align_bytes=64)
@@ -183,67 +173,48 @@ def tile_picked_deliver_gelu_po_kernel(
         out_scale = sb.tile([P, S], U8, name="out_scale", align_bytes=64)
         result = [sb.tile([P, PACK, CHUNK], F32, name=f"result{c}", align_bytes=64) for c in range(CHUNKS)]
         result_bf = [sb.tile([P, HALF, PACK], BF16, name=f"result_bf{h}", align_bytes=64) for h in range(2)]
-
-        def rounded(c):
-            return result_bf[c // 2][:, c % 2 * CHUNK : (c % 2 + 1) * CHUNK, :]
-
-        def second_product(c, planes, bank):
-            acc = psum.tile([P, len(planes), CHUNK], F32, name=f"acc{bank}", tag=f"bank{bank}")
-            for e, t in enumerate(planes):
-                nc.tensor.matmul_mx(
-                    out=acc[:, e, :],
-                    lhsT=w2_codes[:, t * P : (t + 1) * P].bitcast(FP8X4),
-                    lhsT_scale=w2_scale[t // 3][:, t % 3 * P : (t % 3 + 1) * P],
-                    rhs=z_codes[:, chunk[c]].bitcast(FP8X4),
-                    rhs_scale=z_scale[:, chunk[c]],
-                    start=True,
-                    stop=True,
-                )
-            return acc
-
-        def empty(copy, acc, c, planes):
-            rows = slice(planes[0], planes[-1] + 1)
-            copy(out=result[c][:, rows, :], in_=acc[:])
-            nc.sync.dma_start(out=out_rows[:, rows, chunk[c]], in_=result[c][:, rows, :])
+        for c in range(CHUNKS):
+            by_pairs = c < CHUNKS // 2
+            for u in range(2):
+                pair = slice(2 * u, 2 * u + 2)
+                acc = psum.tile([P, 2, CHUNK], F32, name=f"acc{c}_{u}", tag=f"bank{2 * c + u}")
+                for e in range(2):
+                    t = 2 * u + e
+                    nc.tensor.matmul_mx(
+                        out=acc[:, e, :],
+                        lhsT=w2_codes[:, t * P : (t + 1) * P].bitcast(FP8X4),
+                        lhsT_scale=w2_scale[:, t * P : (t + 1) * P],
+                        rhs=z_codes[:, chunk[c]].bitcast(FP8X4),
+                        rhs_scale=z_scale[:, chunk[c]],
+                        start=True,
+                        stop=True,
+                    )
+                copy = nc.vector.tensor_copy if (c, u) in BANKS_ON_VECTOR else nc.scalar.copy
+                copy(out=result[c][:, pair, :], in_=acc[:])
+                if by_pairs:
+                    nc.sync.dma_start(out=out_rows[:, pair, chunk[c]], in_=result[c][:, pair, :])
+            if not by_pairs:
+                nc.sync.dma_start(out=out_rows[:, :, chunk[c]], in_=result[c][:])
 
         def interleave(c):
-            nc.vector.tensor_copy(
-                out=rounded(c).rearrange("p (a i) t -> p a t i", i=4),
+            copy = nc.scalar.copy if c == CHUNK_ON_SCALAR else nc.vector.tensor_copy
+            copy(
+                out=result_bf[c // 2][:, chunk[c % 2], :].rearrange("p (a i) t -> p a t i", i=4),
                 in_=result[c][:].rearrange("p t (a i) -> p a t i", i=4),
             )
 
-        def interleave_bank(copy, acc, c):
-            copy(out=rounded(c), in_=acc[:].rearrange("p t n -> p n t"))
-
-        def quantise_out(c, count):
-            span = slice(c * CHUNK, (c + count) * CHUNK)
-            at = c % 2 * CHUNK
+        def quantise_out(h, part):
+            tokens = slice(h * HALF + part.start, h * HALF + part.stop)
             nc.vector.quantize_mx(
-                out=out_codes[:, span].bitcast(FP8X4),
-                scales=out_scale[:, span],
-                in_=result_bf[c // 2][:, at : at + count * CHUNK, :].rearrange("p n t -> p (n t)"),
+                out=out_codes[:, tokens].bitcast(FP8X4), scales=out_scale[:, tokens], in_=result_bf[h][:, part, :].rearrange("p n t -> p (n t)")
             )
 
-        def store_words(queue, c, count):
-            span = slice(c * CHUNK, (c + count) * CHUNK)
-            queue.dma_start(out=out_words[:, span], in_=out_codes[:, span])
-
-        every = range(PACK)
-        empty(nc.scalar.copy, second_product(0, (0, 1), 0), 0, (0, 1))
-        empty(nc.vector.tensor_copy, second_product(0, (2, 3), 1), 0, (2, 3))
-        empty(nc.scalar.copy, second_product(1, (0, 1), 2), 1, (0, 1))
-        empty(nc.vector.tensor_copy, second_product(1, (2, 3), 3), 1, (2, 3))
-        empty(nc.scalar.copy, second_product(2, every, 4), 2, every)
-        final = second_product(3, every, 5)
-        empty(nc.scalar.copy, final, 3, every)
-        interleave_bank(nc.scalar.copy, final, 3)
-        for c in range(3):
-            interleave(c)
-        quantise_out(0, 2)
-        store_words(nc.sync, 0, 2)
-        quantise_out(2, 1)
-        quantise_out(3, 1)
-        store_words(nc.sync, 2, 2)
+        for h, parts in enumerate(([halves[0]], chunk[0:2])):
+            interleave(2 * h)
+            interleave(2 * h + 1)
+            for part in parts:
+                quantise_out(h, part)
+            nc.sync.dma_start(out=out_words[:, halves[h]], in_=out_codes[:, halves[h]])
         for q in range(4):
             queue = nc.scalar if q % 2 else nc.sync
             queue.dma_start(out=out_2[0, 4 * q : 4 * q + 4, :].bitcast(I32), in_=out_scale[32 * q : 32 * q + 4, :].bitcast(I32))

@@ -54,11 +54,11 @@ def tile_picked_deliver_gelu_po_kernel(
         nc.gpsimd.memset(w2_raw_scales[:].bitcast(I32), 0)
 
         w1_rows = w1.rearrange("(p j) c -> p j c", j=PACK)
-        w1_raw = [sb.tile([P, PACK, H // 2], F32, name=f"w1_raw{u}", align_bytes=64) for u in range(2)]
-        nc.sync.dma_start(out=w1_raw[0][:], in_=w1_rows[:, :, 0 : H // 2])
+        w1_raw = [sb.tile([P, 2, H], F32, name=f"w1_raw{u}", align_bytes=64) for u in range(2)]
+        nc.sync.dma_start(out=w1_raw[0][:], in_=w1_rows[:, 0:2, :])
         load_scale_rows(nc.sync, x_table_scales, x_scales)
         nc.sync.dma_start(offs_sb[:], offs)
-        nc.sync.dma_start(out=w1_raw[1][:], in_=w1_rows[:, :, H // 2 : H])
+        nc.sync.dma_start(out=w1_raw[1][:], in_=w1_rows[:, 2:4, :])
         nc.sync.dma_start(out=x_table[:], in_=as_words(x_words))
         nc.sync.dma_start(out=w2_raw[:], in_=as_words(w2_words))
         load_scale_rows(nc.sync, w2_raw_scales, w2_scales)
@@ -69,8 +69,8 @@ def tile_picked_deliver_gelu_po_kernel(
         x_scale = sb.tile([P, S], U8, name="x_scale", align_bytes=64)
         for u in range(2):
             nc.vector.tensor_copy(
-                out=w1_bf[:, :, u * P // 2 : (u + 1) * P // 2, :].rearrange("p t m j -> p m t j"),
-                in_=w1_raw[u][:].rearrange("p j (m t) -> p m t j", t=PACK),
+                out=w1_bf[:, :, :, 2 * u : 2 * u + 2].rearrange("p t m j -> p m j t"),
+                in_=w1_raw[u][:].rearrange("p j (m t) -> p m j t", t=PACK),
             )
             if u == 0:
                 nc.vector.tensor_copy(x_scale[:], x_table_scales[:].indirect(offs_sb[:]))

@@ -13,6 +13,7 @@ U16 = mybir.dt.uint16
 U8 = mybir.dt.uint8
 FP8X4 = mybir.dt.float8_e4m3fn_x4
 GELU = mybir.ActivationFunctionType.Gelu_apprx_tanh
+COPY = mybir.ActivationFunctionType.Copy
 
 P = 128
 PACK = 4
@@ -20,7 +21,7 @@ LIST_ROWS = 16
 HALF = S // 2
 CHUNK = 128
 CHUNKS = S // CHUNK
-ORDER = (2, 3, 0, 1)
+ORDER = (2, 0, 3, 1)
 BANKS_ON_VECTOR = ((0, 1), (2, 1))
 CHUNK_ON_SCALAR = 2
 
@@ -100,33 +101,36 @@ def tile_picked_deliver_gelu_po_kernel(
         chunk = [slice(c * CHUNK, (c + 1) * CHUNK) for c in range(CHUNKS)]
         first_parts = [halves[0], chunk[2], chunk[3]]
         first_banks = [psum.tile([P, part.stop - part.start], F32, name=f"y_first{i}", tag=f"bank{i}") for i, part in enumerate(first_parts)]
-        y_bank = {t: psum.tile([P, S], F32, name=f"y{t}", tag=f"bank{len(first_parts) + i}") for i, t in enumerate(ORDER[1:])}
+        second_banks = [psum.tile([P, HALF], F32, name=f"y_second{h}", tag=f"bank{3 + h}") for h in range(2)]
+        third_banks = [psum.tile([P, HALF], F32, name=f"y_third{h}", tag=f"bank{5 + h}") for h in range(2)]
+        last_bank = psum.tile([P, S], F32, name="y_last", tag="bank7")
         first_product(first_banks[0][:], first, first_parts[0])
-        first_product(y_bank[second][:, halves[0]], second, halves[0])
+        first_product(second_banks[0][:], second, halves[0])
         for bank, part in zip(first_banks[1:], first_parts[1:]):
             first_product(bank[:], first, part)
-        first_product(y_bank[second][:, halves[1]], second, halves[1])
-        for t in (third, last):
-            for half in halves:
-                first_product(y_bank[t][:, half], t, half)
+        first_product(second_banks[1][:], second, halves[1])
+        for bank, half in zip(third_banks, halves):
+            first_product(bank[:], third, half)
+        for half in halves:
+            first_product(last_bank[:, half], last, half)
 
         first_gelu = sb.tile([P, S], F32, name="first_gelu", align_bytes=64)
         for bank, part in zip(first_banks, first_parts):
             nc.scalar.activation(first_gelu[:, part], bank[:], GELU)
 
-        w2_codes = sb.tile([P, N], I32, name="w2_codes", align_bytes=64)
-        w2_scale = sb.tile([P, N], U8, name="w2_scale", align_bytes=64)
-        for dealt, raw in ((w2_codes, w2_raw), (w2_scale, w2_raw_scales)):
+        def deal(dealt, raw):
             nc.vector.tensor_copy(out=dealt[:].rearrange("p (t m) -> p m t", t=PACK), in_=raw[:].rearrange("p (m t) -> p m t", t=PACK))
 
-        z = [sb.tile([P, S], F32, name=f"z{t}", tag="w2_raw_scales" if t == first else f"z{t}", align_bytes=64) for t in range(PACK)]
+        w2_codes = sb.tile([P, N], I32, name="w2_codes", align_bytes=64)
+        deal(w2_codes, w2_raw)
+
+        z = [sb.tile([P, S], F32, name=f"z{t}", align_bytes=64) for t in range(PACK)]
         fetched = [sb.tile([P, V], F32, name=f"fetched{t}", tag="w2_raw" if t == first else f"fetched{t}", align_bytes=64) for t in range(PACK)]
         message = {t: sb.tile([P, V], F32, name=f"message{t}", align_bytes=64) for t in ORDER[1:]}
         message[first] = fetched[first]
-        z_bf = sb.tile([P, S, PACK], BF16, name="z_bf", align_bytes=64)
 
-        def fetch(t, window):
-            nc.vector.tensor_copy(fetched[t][:], window[:].indirect(src_sb[:]))
+        def fetch(t):
+            nc.scalar.activation(fetched[t][:], z[t][:].indirect(src_sb[:]), COPY)
 
         def activate(t):
             nc.scalar.activation(message[t][:], fetched[t][:], GELU)
@@ -134,28 +138,41 @@ def tile_picked_deliver_gelu_po_kernel(
         def deliver(t):
             nc.vector.tensor_copy(z[t][:].indirect(dst_sb[:]), message[t][:])
 
-        nc.scalar.copy(out=z[second][:], in_=y_bank[second][:])
-        for bank, part in zip(first_banks, first_parts):
+        nc.vector.tensor_copy(out=z[second][:, halves[0]], in_=second_banks[0][:])
+        nc.vector.tensor_copy(out=z[first][:, halves[0]], in_=first_banks[0][:])
+        nc.vector.tensor_copy(fetched[first][:], first_gelu[:].indirect(src_sb[:]))
+        for bank, part in zip(first_banks[1:], first_parts[1:]):
             nc.scalar.copy(out=z[first][:, part], in_=bank[:])
-        for t in (third, last):
-            nc.scalar.copy(out=z[t][:], in_=y_bank[t][:])
-
-        fetch(first, first_gelu)
-        fetch(second, z[second])
         deliver(first)
-        fetch(third, z[third])
-        fetch(last, z[last])
-        for step in (activate, deliver):
-            for t in ORDER[1:]:
-                step(t)
-        for t in (first, second):
-            nc.scalar.copy(out=z_bf[:, :, t], in_=z[t][:])
+        nc.scalar.copy(out=z[second][:, halves[1]], in_=second_banks[1][:])
+        nc.scalar.copy(out=z[third][:, halves[0]], in_=third_banks[0][:])
+        fetch(second)
+        nc.scalar.copy(out=z[third][:, halves[1]], in_=third_banks[1][:])
+        activate(second)
+        deliver(second)
+        fetch(third)
+        nc.scalar.copy(out=z[last][:], in_=last_bank[:])
+        activate(third)
+        deliver(third)
+        fetch(last)
 
-        nc.scalar.copy(
-            out=z_bf[:, halves[0], third : last + 1],
-            in_=z[third][:, halves[0]].rearrange("p (n o) -> p n o", o=1).to_broadcast([P, HALF, 2]),
-        )
-        nc.scalar.copy(out=z_bf[:, halves[1], third], in_=z[third][:, halves[1]])
+        activate(last)
+        deliver(last)
+        w2_scale = sb.tile([P, N], U8, name="w2_scale", tag=f"fetched{last}", align_bytes=64)
+        deal(w2_scale, w2_raw_scales)
+
+        z_bf = sb.tile([P, S, PACK], BF16, name="z_bf", align_bytes=64)
+        for t in (first, second):
+            nc.gpsimd.tensor_scalar(
+                out=z_bf[:, :, t : t + 2],
+                in0=z[t][:].rearrange("p (n o) -> p n o", o=1).to_broadcast([P, S, 2]),
+                scalar1=1.0,
+                scalar2=0.0,
+                op0=mybir.AluOpType.mult,
+                op1=mybir.AluOpType.add,
+            )
+        for half in halves:
+            nc.scalar.copy(out=z_bf[:, half, third], in_=z[third][:, half])
         for c in range(CHUNKS):
             copy = nc.vector.tensor_copy if c < CHUNKS // 2 else nc.scalar.copy
             copy(out=z_bf[:, chunk[c], last], in_=z[last][:, chunk[c]])

@@ -161,16 +161,19 @@ def tile_picked_deliver_gelu_po_kernel(
         w2_scale = sb.tile([P, N], U8, name="w2_scale", tag=f"fetched{last}", align_bytes=64)
         deal(w2_scale, w2_raw_scales)
 
-        z_bf = sb.tile([P, S, PACK], BF16, name="z_bf", align_bytes=64)
+        z_bf = sb.tile([P, S, PACK], BF16, name="z_bf", tag=f"fetched{second}", align_bytes=64)
+        shared = S - CHUNK
         for t in (first, second):
             nc.gpsimd.tensor_scalar(
-                out=z_bf[:, :, t : t + 2],
-                in0=z[t][:].rearrange("p (n o) -> p n o", o=1).to_broadcast([P, S, 2]),
+                out=z_bf[:, 0:shared, t : t + 2],
+                in0=z[t][:, 0:shared].rearrange("p (n o) -> p n o", o=1).to_broadcast([P, shared, 2]),
                 scalar1=1.0,
                 scalar2=0.0,
                 op0=mybir.AluOpType.mult,
                 op1=mybir.AluOpType.add,
             )
+        for t in (first, second):
+            nc.scalar.copy(out=z_bf[:, shared:, t], in_=z[t][:, shared:])
         for half in halves:
             nc.scalar.copy(out=z_bf[:, half, third], in_=z[third][:, half])
         for c in range(CHUNKS):

@@ -62,8 +62,8 @@ def tile_picked_deliver_gelu_po_kernel(
         nc.sync.dma_start(out=w1_raw[1][:], in_=w1_rows[:, 2:4, :])
         nc.sync.dma_start(out=x_table[:], in_=as_words(x_words))
         nc.sync.dma_start(out=w2_raw[:], in_=as_words(w2_words))
-        load_scale_rows(nc.sync, w2_raw_scales, w2_scales)
         nc.sync.dma_start(src_sb[:], src)
+        load_scale_rows(nc.sync, w2_raw_scales, w2_scales)
         nc.sync.dma_start(dst_sb[:], dst)
 
         w1_bf = sb.tile([P, PACK, P, PACK], BF16, name="w1_bf", align_bytes=64)
@@ -79,10 +79,11 @@ def tile_picked_deliver_gelu_po_kernel(
         w1_scale = sb.tile([P, H], U8, name="w1_scale", align_bytes=64)
         nc.vector.quantize_mx(out=w1_codes[:].bitcast(FP8X4), scales=w1_scale[:], in_=w1_bf[:].rearrange("p t m j -> p (t m j)"))
 
-        columns = HALF // LIST_ROWS
         x_codes = [sb.tile([P, HALF], U32, name=f"x_codes{h}", align_bytes=64) for h in range(2)]
-        for h in range(2):
-            nc.vector.tensor_copy(x_codes[h][:], x_table[:].bitcast(U32).indirect(offs_sb[:, h * columns : (h + 1) * columns]))
+        for start, count in ((0, HALF), (HALF, CHUNK), (HALF + CHUNK, CHUNK)):
+            h, at = divmod(start, HALF)
+            offsets = offs_sb[:, start // LIST_ROWS : (start + count) // LIST_ROWS]
+            nc.vector.tensor_copy(x_codes[h][:, at : at + count], x_table[:].bitcast(U32).indirect(offsets))
 
         def first_product(acc, t, tokens):
             h, at = divmod(tokens.start, HALF)
@@ -141,6 +142,8 @@ def tile_picked_deliver_gelu_po_kernel(
         nc.vector.tensor_copy(out=z[second][:, halves[0]], in_=second_banks[0][:])
         nc.vector.tensor_copy(out=z[first][:, halves[0]], in_=first_banks[0][:])
         nc.vector.tensor_copy(fetched[first][:], first_gelu[:].indirect(src_sb[:]))
+        w2_scale = sb.tile([P, N], U8, name="w2_scale", align_bytes=64)
+        deal(w2_scale, w2_raw_scales)
         for bank, part in zip(first_banks[1:], first_parts[1:]):
             nc.scalar.copy(out=z[first][:, part], in_=bank[:])
         deliver(first)
@@ -158,11 +161,9 @@ def tile_picked_deliver_gelu_po_kernel(
 
         activate(last)
         deliver(last)
-        w2_scale = sb.tile([P, N], U8, name="w2_scale", tag=f"fetched{last}", align_bytes=64)
-        deal(w2_scale, w2_raw_scales)
 
         z_bf = sb.tile([P, S, PACK], BF16, name="z_bf", tag=f"fetched{second}", align_bytes=64)
-        shared = S - CHUNK
+        shared = S
         for t in (first, second):
             nc.gpsimd.tensor_scalar(
                 out=z_bf[:, 0:shared, t : t + 2],
@@ -172,8 +173,6 @@ def tile_picked_deliver_gelu_po_kernel(
                 op0=mybir.AluOpType.mult,
                 op1=mybir.AluOpType.add,
             )
-        for t in (first, second):
-            nc.scalar.copy(out=z_bf[:, shared:, t], in_=z[t][:, shared:])
         for half in halves:
             nc.scalar.copy(out=z_bf[:, half, third], in_=z[third][:, half])
         for c in range(CHUNKS):

@@ -103,15 +103,14 @@ def tile_picked_deliver_gelu_po_kernel(
         first_parts = [halves[0], chunk[2], chunk[3]]
         first_banks = [psum.tile([P, part.stop - part.start], F32, name=f"y_first{i}", tag=f"bank{i}") for i, part in enumerate(first_parts)]
         second_banks = [psum.tile([P, HALF], F32, name=f"y_second{h}", tag=f"bank{3 + h}") for h in range(2)]
-        third_banks = [psum.tile([P, HALF], F32, name=f"y_third{h}", tag=f"bank{5 + h}") for h in range(2)]
-        last_bank = psum.tile([P, S], F32, name="y_last", tag="bank7")
+        third_banks = [psum.tile([P, HALF], F32, name="y_third0", tag="bank5")]
+        last_bank = psum.tile([P, S], F32, name="y_last", tag="bank6")
         first_product(first_banks[0][:], first, first_parts[0])
         first_product(second_banks[0][:], second, halves[0])
         for bank, part in zip(first_banks[1:], first_parts[1:]):
             first_product(bank[:], first, part)
         first_product(second_banks[1][:], second, halves[1])
-        for bank, half in zip(third_banks, halves):
-            first_product(bank[:], third, half)
+        first_product(third_banks[0][:], third, halves[0])
         for half in halves:
             first_product(last_bank[:, half], last, half)
 
@@ -125,7 +124,7 @@ def tile_picked_deliver_gelu_po_kernel(
         w2_codes = sb.tile([P, N], I32, name="w2_codes", align_bytes=64)
         deal(w2_codes, w2_raw)
 
-        z = [sb.tile([P, S], F32, name=f"z{t}", align_bytes=64) for t in range(PACK)]
+        z = {t: sb.tile([P, S], F32, name=f"z{t}", align_bytes=64) for t in (first, second, third)}
         fetched = [sb.tile([P, V], F32, name=f"fetched{t}", tag="w2_raw" if t == first else f"fetched{t}", align_bytes=64) for t in range(PACK)]
         message = {t: sb.tile([P, V], F32, name=f"message{t}", align_bytes=64) for t in ORDER[1:]}
         message[first] = fetched[first]
@@ -144,11 +143,14 @@ def tile_picked_deliver_gelu_po_kernel(
         nc.vector.tensor_copy(fetched[first][:], first_gelu[:].indirect(src_sb[:]))
         w2_scale = sb.tile([P, N], U8, name="w2_scale", align_bytes=64)
         deal(w2_scale, w2_raw_scales)
+        z[last] = sb.tile([P, S], F32, name=f"z{last}", tag="w2_raw_scales", align_bytes=64)
         for bank, part in zip(first_banks[1:], first_parts[1:]):
             nc.scalar.copy(out=z[first][:, part], in_=bank[:])
         deliver(first)
         nc.scalar.copy(out=z[second][:, halves[1]], in_=second_banks[1][:])
         nc.scalar.copy(out=z[third][:, halves[0]], in_=third_banks[0][:])
+        third_banks.append(psum.tile([P, HALF], F32, name="y_third1", tag="bank4"))
+        first_product(third_banks[1][:], third, halves[1])
         fetch(second)
         nc.scalar.copy(out=z[third][:, halves[1]], in_=third_banks[1][:])
         activate(second)

@@ -124,8 +124,8 @@ def tile_picked_deliver_gelu_po_kernel(
         w2_codes = sb.tile([P, N], I32, name="w2_codes", align_bytes=64)
         deal(w2_codes, w2_raw)
 
-        z = {t: sb.tile([P, S], F32, name=f"z{t}", align_bytes=64) for t in (first, second, third)}
-        fetched = [sb.tile([P, V], F32, name=f"fetched{t}", tag="w2_raw" if t == first else f"fetched{t}", align_bytes=64) for t in range(PACK)]
+        z = {t: sb.tile([P, S], F32, name=f"z{t}", tag="w2_raw" if t == first else f"z{t}", align_bytes=64) for t in (first, second, third)}
+        fetched = [sb.tile([P, V], F32, name=f"fetched{t}", tag=f"fetched{t}", align_bytes=64) for t in range(PACK)]
         message = {t: sb.tile([P, V], F32, name=f"message{t}", align_bytes=64) for t in ORDER[1:]}
         message[first] = fetched[first]
 
@@ -139,12 +139,11 @@ def tile_picked_deliver_gelu_po_kernel(
             nc.vector.tensor_copy(z[t][:].indirect(dst_sb[:]), message[t][:])
 
         nc.vector.tensor_copy(out=z[second][:, halves[0]], in_=second_banks[0][:])
-        nc.vector.tensor_copy(out=z[first][:, halves[0]], in_=first_banks[0][:])
         nc.vector.tensor_copy(fetched[first][:], first_gelu[:].indirect(src_sb[:]))
         w2_scale = sb.tile([P, N], U8, name="w2_scale", align_bytes=64)
         deal(w2_scale, w2_raw_scales)
         z[last] = sb.tile([P, S], F32, name=f"z{last}", tag="w2_raw_scales", align_bytes=64)
-        for bank, part in zip(first_banks[1:], first_parts[1:]):
+        for bank, part in zip(first_banks, first_parts):
             nc.scalar.copy(out=z[first][:, part], in_=bank[:])
         deliver(first)
         nc.scalar.copy(out=z[second][:, halves[1]], in_=second_banks[1][:])
@@ -165,21 +164,21 @@ def tile_picked_deliver_gelu_po_kernel(
         deliver(last)
 
         z_bf = sb.tile([P, S, PACK], BF16, name="z_bf", tag=f"fetched{second}", align_bytes=64)
-        shared = S
+
+        def round_on_gpsimd(out, values):
+            nc.gpsimd.tensor_scalar(out=out, in0=values, scalar1=1.0, scalar2=0.0, op0=mybir.AluOpType.mult, op1=mybir.AluOpType.add)
+
         for t in (first, second):
-            nc.gpsimd.tensor_scalar(
-                out=z_bf[:, 0:shared, t : t + 2],
-                in0=z[t][:, 0:shared].rearrange("p (n o) -> p n o", o=1).to_broadcast([P, shared, 2]),
-                scalar1=1.0,
-                scalar2=0.0,
-                op0=mybir.AluOpType.mult,
-                op1=mybir.AluOpType.add,
-            )
-        for half in halves:
-            nc.scalar.copy(out=z_bf[:, half, third], in_=z[third][:, half])
-        for c in range(CHUNKS):
-            copy = nc.vector.tensor_copy if c < CHUNKS // 2 else nc.scalar.copy
-            copy(out=z_bf[:, chunk[c], last], in_=z[last][:, chunk[c]])
+            round_on_gpsimd(z_bf[:, :, t : t + 2], z[t][:].rearrange("p (n o) -> p n o", o=1).to_broadcast([P, S, 2]))
+        nc.scalar.copy(out=z_bf[:, halves[0], third], in_=z[third][:, halves[0]])
+        round_on_gpsimd(z_bf[:, halves[1], third], z[third][:, halves[1]])
+        middle = CHUNK // 2
+        for copy, parts in (
+            (nc.vector.tensor_copy, (slice(0, middle), chunk[1])),
+            (nc.scalar.copy, (slice(middle, CHUNK), chunk[2], chunk[3])),
+        ):
+            for part in parts:
+                copy(out=z_bf[:, part, last], in_=z[last][:, part])
 
         z_codes = sb.tile([P, S], U32, name="z_codes", align_bytes=64)
         z_scale = sb.tile([P, S], U8, name="z_scale", align_bytes=64)

@@ -62,8 +62,8 @@ def tile_picked_deliver_gelu_po_kernel(
         nc.sync.dma_start(out=w1_raw[1][:], in_=w1_rows[:, 2:4, :])
         nc.sync.dma_start(out=x_table[:], in_=as_words(x_words))
         nc.sync.dma_start(out=w2_raw[:], in_=as_words(w2_words))
-        nc.sync.dma_start(src_sb[:], src)
         load_scale_rows(nc.sync, w2_raw_scales, w2_scales)
+        nc.sync.dma_start(src_sb[:], src)
         nc.sync.dma_start(dst_sb[:], dst)
 
         w1_bf = sb.tile([P, PACK, P, PACK], BF16, name="w1_bf", align_bytes=64)
@@ -114,7 +114,7 @@ def tile_picked_deliver_gelu_po_kernel(
         for half in halves:
             first_product(last_bank[:, half], last, half)
 
-        first_gelu = sb.tile([P, S], F32, name="first_gelu", align_bytes=64)
+        first_gelu = sb.tile([P, S], F32, name="first_gelu", tag="first_gelu", align_bytes=64)
         for bank, part in zip(first_banks, first_parts):
             nc.scalar.activation(first_gelu[:, part], bank[:], GELU)
 
@@ -123,6 +123,8 @@ def tile_picked_deliver_gelu_po_kernel(
 
         w2_codes = sb.tile([P, N], I32, name="w2_codes", align_bytes=64)
         deal(w2_codes, w2_raw)
+        w2_scale = sb.tile([P, N], U8, name="w2_scale", align_bytes=64)
+        deal(w2_scale, w2_raw_scales)
 
         z = {t: sb.tile([P, S], F32, name=f"z{t}", tag="w2_raw" if t == first else f"z{t}", align_bytes=64) for t in (first, second, third)}
         fetched = [sb.tile([P, V], F32, name=f"fetched{t}", tag=f"fetched{t}", align_bytes=64) for t in range(PACK)]
@@ -140,9 +142,7 @@ def tile_picked_deliver_gelu_po_kernel(
 
         nc.vector.tensor_copy(out=z[second][:, halves[0]], in_=second_banks[0][:])
         nc.vector.tensor_copy(fetched[first][:], first_gelu[:].indirect(src_sb[:]))
-        w2_scale = sb.tile([P, N], U8, name="w2_scale", align_bytes=64)
-        deal(w2_scale, w2_raw_scales)
-        z[last] = sb.tile([P, S], F32, name=f"z{last}", tag="w2_raw_scales", align_bytes=64)
+        z[last] = sb.tile([P, S], F32, name=f"z{last}", tag="first_gelu", align_bytes=64)
         for bank, part in zip(first_banks, first_parts):
             nc.scalar.copy(out=z[first][:, part], in_=bank[:])
         deliver(first)

@@ -22,8 +22,7 @@ HALF = S // 2
 CHUNK = 128
 CHUNKS = S // CHUNK
 ORDER = (2, 0, 3, 1)
-BANKS_ON_VECTOR = ((0, 1), (2, 1))
-CHUNK_ON_SCALAR = 2
+BANKS_ON_VECTOR = ((0, 1),)
 
 
 def as_words(packed):
@@ -182,9 +181,9 @@ def tile_picked_deliver_gelu_po_kernel(
 
         z_codes = sb.tile([P, S], U32, name="z_codes", align_bytes=64)
         z_scale = sb.tile([P, S], U8, name="z_scale", align_bytes=64)
-        for c in range(CHUNKS):
+        for part in (chunk[0], chunk[1], halves[1]):
             nc.vector.quantize_mx(
-                out=z_codes[:, chunk[c]].bitcast(FP8X4), scales=z_scale[:, chunk[c]], in_=z_bf[:, chunk[c], :].rearrange("p n t -> p (n t)")
+                out=z_codes[:, part].bitcast(FP8X4), scales=z_scale[:, part], in_=z_bf[:, part, :].rearrange("p n t -> p (n t)")
             )
 
         out_rows = out_0.rearrange("(p t) n -> p t n", t=PACK)
@@ -217,8 +216,7 @@ def tile_picked_deliver_gelu_po_kernel(
                 nc.sync.dma_start(out=out_rows[:, :, chunk[c]], in_=result[c][:])
 
         def interleave(c):
-            copy = nc.scalar.copy if c == CHUNK_ON_SCALAR else nc.vector.tensor_copy
-            copy(
+            nc.vector.tensor_copy(
                 out=result_bf[c // 2][:, chunk[c % 2], :].rearrange("p (a i) t -> p a t i", i=4),
                 in_=result[c][:].rearrange("p t (a i) -> p a t i", i=4),
             )

@@ -21,6 +21,7 @@ LIST_ROWS = 16
 HALF = S // 2
 CHUNK = 128
 CHUNKS = S // CHUNK
+SCALE_ROWS_AT = P - K // 32
 ORDER = (2, 0, 3, 1)
 BANKS_ON_VECTOR = ((0, 1),)
 
@@ -40,40 +41,47 @@ def tile_picked_deliver_gelu_po_kernel(
     nc = tc.nc
     with ExitStack() as ctx:
         sb = ctx.enter_context(tc.tile_pool(name="sb", bufs=1))
+        reused = ctx.enter_context(tc.tile_pool(name="reused", bufs=1))
         psum = ctx.enter_context(tc.psum_pool(name="psum", bufs=1))
 
         offs_sb = sb.tile([P, S // LIST_ROWS], U16, name="offs_sb")
         src_sb = sb.tile([P, V // LIST_ROWS], U16, name="src_sb")
         dst_sb = sb.tile([P, V // LIST_ROWS], U16, name="dst_sb")
         x_table = sb.tile([P, T], I32, name="x_table", align_bytes=64)
-        x_table_scales = sb.tile([P, T], U8, name="x_table_scales", align_bytes=64)
-        w2_raw = sb.tile([P, N], I32, name="w2_raw", tag="w2_raw", align_bytes=64)
-        w2_raw_scales = sb.tile([P, N], U8, name="w2_raw_scales", tag="w2_raw_scales", align_bytes=64)
+        x_table_scales = reused.tile([P, T], U8, name="x_table_scales", offset=0, align_bytes=64)
+        x_scale = sb.tile([P, S], U8, name="x_scale", align_bytes=64)
 
-        nc.vector.memset(x_table_scales[:].bitcast(I32), 0)
-        nc.gpsimd.memset(w2_raw_scales[:].bitcast(I32), 0)
+        nc.vector.memset(x_table_scales[0:96, :].bitcast(I32), 0)
+        nc.vector.memset(x_table_scales[96:SCALE_ROWS_AT, :].bitcast(I32), 0)
+        nc.vector.memset(x_scale[:].bitcast(I32), 0)
 
         w1_rows = w1.rearrange("(p j) c -> p j c", j=PACK)
         w1_raw = [sb.tile([P, 2, H], F32, name=f"w1_raw{u}", align_bytes=64) for u in range(2)]
-        nc.sync.dma_start(out=w1_raw[0][:], in_=w1_rows[:, 0:2, :])
-        load_scale_rows(nc.sync, x_table_scales, x_scales)
+        nc.sync.dma_start(out=x_table_scales[SCALE_ROWS_AT:P, :].bitcast(I32), in_=x_scales[0].bitcast(I32))
         nc.sync.dma_start(offs_sb[:], offs)
+        nc.sync.dma_start(out=w1_raw[0][:], in_=w1_rows[:, 0:2, :])
         nc.sync.dma_start(out=w1_raw[1][:], in_=w1_rows[:, 2:4, :])
         nc.sync.dma_start(out=x_table[:], in_=as_words(x_words))
-        nc.sync.dma_start(out=w2_raw[:], in_=as_words(w2_words))
-        load_scale_rows(nc.sync, w2_raw_scales, w2_scales)
         nc.sync.dma_start(src_sb[:], src)
         nc.sync.dma_start(dst_sb[:], dst)
 
+        picked_scales = sb.tile([P, S], U8, name="picked_scales", align_bytes=64)
+        nc.vector.tensor_copy(picked_scales[:], x_table_scales[:].indirect(offs_sb[:]))
+        for q in range(4):
+            rows = slice(SCALE_ROWS_AT + 4 * q, SCALE_ROWS_AT + 4 * q + 4)
+            nc.scalar.dma_start(out=x_scale[32 * q : 32 * q + 4, :].bitcast(I32), in_=picked_scales[rows, :].bitcast(I32))
+        w2_raw = reused.tile([P, N], I32, name="w2_raw", offset=T - 64, align_bytes=64)
+        w2_raw_scales = reused.tile([P, N], U8, name="w2_raw_scales", offset=0, align_bytes=64)
+        nc.sync.dma_start(out=w2_raw[:], in_=as_words(w2_words))
+        nc.vector.memset(w2_raw_scales[:].bitcast(I32), 0)
+        load_scale_rows(nc.sync, w2_raw_scales, w2_scales)
+
         w1_bf = sb.tile([P, PACK, P, PACK], BF16, name="w1_bf", align_bytes=64)
-        x_scale = sb.tile([P, S], U8, name="x_scale", align_bytes=64)
         for u in range(2):
             nc.vector.tensor_copy(
                 out=w1_bf[:, :, :, 2 * u : 2 * u + 2].rearrange("p t m j -> p m j t"),
                 in_=w1_raw[u][:].rearrange("p j (m t) -> p m j t", t=PACK),
             )
-            if u == 0:
-                nc.vector.tensor_copy(x_scale[:], x_table_scales[:].indirect(offs_sb[:]))
         w1_codes = sb.tile([P, H], U32, name="w1_codes", align_bytes=64)
         w1_scale = sb.tile([P, H], U8, name="w1_scale", align_bytes=64)
         nc.vector.quantize_mx(out=w1_codes[:].bitcast(FP8X4), scales=w1_scale[:], in_=w1_bf[:].rearrange("p t m j -> p (t m j)"))
@@ -102,16 +110,12 @@ def tile_picked_deliver_gelu_po_kernel(
         first_parts = [halves[0], chunk[2], chunk[3]]
         first_banks = [psum.tile([P, part.stop - part.start], F32, name=f"y_first{i}", tag=f"bank{i}") for i, part in enumerate(first_parts)]
         second_banks = [psum.tile([P, HALF], F32, name=f"y_second{h}", tag=f"bank{3 + h}") for h in range(2)]
-        third_banks = [psum.tile([P, HALF], F32, name="y_third0", tag="bank5")]
         last_bank = psum.tile([P, S], F32, name="y_last", tag="bank6")
         first_product(first_banks[0][:], first, first_parts[0])
         first_product(second_banks[0][:], second, halves[0])
         for bank, part in zip(first_banks[1:], first_parts[1:]):
             first_product(bank[:], first, part)
         first_product(second_banks[1][:], second, halves[1])
-        first_product(third_banks[0][:], third, halves[0])
-        for half in halves:
-            first_product(last_bank[:, half], last, half)
 
         first_gelu = sb.tile([P, S], F32, name="first_gelu", tag="first_gelu", align_bytes=64)
         for bank, part in zip(first_banks, first_parts):
@@ -122,11 +126,11 @@ def tile_picked_deliver_gelu_po_kernel(
 
         w2_codes = sb.tile([P, N], I32, name="w2_codes", align_bytes=64)
         deal(w2_codes, w2_raw)
-        w2_scale = sb.tile([P, N], U8, name="w2_scale", align_bytes=64)
-        deal(w2_scale, w2_raw_scales)
 
-        z = {t: sb.tile([P, S], F32, name=f"z{t}", tag="w2_raw" if t == first else f"z{t}", align_bytes=64) for t in (first, second, third)}
-        fetched = [sb.tile([P, V], F32, name=f"fetched{t}", tag=f"fetched{t}", align_bytes=64) for t in range(PACK)]
+        z = {t: reused.tile([P, S], F32, name=f"z{t}", offset=at, align_bytes=64) for t, at in ((first, N), (second, N + 4 * S + 4 * V))}
+        z[third] = sb.tile([P, S], F32, name=f"z{third}", align_bytes=64)
+        fetched = {t: sb.tile([P, V], F32, name=f"fetched{t}", tag=f"fetched{t}", align_bytes=64) for t in ORDER[1:]}
+        fetched[first] = reused.tile([P, V], F32, name=f"fetched{first}", offset=N + 4 * S, align_bytes=64)
         message = {t: sb.tile([P, V], F32, name=f"message{t}", align_bytes=64) for t in ORDER[1:]}
         message[first] = fetched[first]
 
@@ -145,6 +149,10 @@ def tile_picked_deliver_gelu_po_kernel(
         for bank, part in zip(first_banks, first_parts):
             nc.scalar.copy(out=z[first][:, part], in_=bank[:])
         deliver(first)
+        third_banks = [psum.tile([P, HALF], F32, name="y_third0", tag="bank0")]
+        first_product(third_banks[0][:], third, halves[0])
+        for half in halves:
+            first_product(last_bank[:, half], last, half)
         nc.scalar.copy(out=z[second][:, halves[1]], in_=second_banks[1][:])
         nc.scalar.copy(out=z[third][:, halves[0]], in_=third_banks[0][:])
         third_banks.append(psum.tile([P, HALF], F32, name="y_third1", tag="bank4"))
@@ -161,6 +169,8 @@ def tile_picked_deliver_gelu_po_kernel(
 
         activate(last)
         deliver(last)
+        w2_scale = sb.tile([P, N], U8, name="w2_scale", tag=f"fetched{last}", align_bytes=64)
+        deal(w2_scale, w2_raw_scales)
 
         z_bf = sb.tile([P, S, PACK], BF16, name="z_bf", tag=f"fetched{second}", align_bytes=64)
 

@@ -179,15 +179,11 @@ def tile_picked_deliver_gelu_po_kernel(
 
         for t in (first, second):
             round_on_gpsimd(z_bf[:, :, t : t + 2], z[t][:].rearrange("p (n o) -> p n o", o=1).to_broadcast([P, S, 2]))
-        nc.scalar.copy(out=z_bf[:, halves[0], third], in_=z[third][:, halves[0]])
-        round_on_gpsimd(z_bf[:, halves[1], third], z[third][:, halves[1]])
-        middle = CHUNK // 2
-        for copy, parts in (
-            (nc.vector.tensor_copy, (slice(0, middle), chunk[1])),
-            (nc.scalar.copy, (slice(middle, CHUNK), chunk[2], chunk[3])),
-        ):
-            for part in parts:
-                copy(out=z_bf[:, part, last], in_=z[last][:, part])
+        for half in halves:
+            nc.scalar.copy(out=z_bf[:, half, third], in_=z[third][:, half])
+        for c, part in enumerate(chunk):
+            copy = nc.vector.tensor_copy if c < CHUNKS // 2 else nc.scalar.copy
+            copy(out=z_bf[:, part, last], in_=z[last][:, part])
 
         z_codes = sb.tile([P, S], U32, name="z_codes", align_bytes=64)
         z_scale = sb.tile([P, S], U8, name="z_scale", align_bytes=64)

@@ -57,7 +57,7 @@ def tile_picked_deliver_gelu_po_kernel(
 
         w1_rows = w1.rearrange("(p j) c -> p j c", j=PACK)
         w1_raw = [sb.tile([P, 2, H], F32, name=f"w1_raw{u}", align_bytes=64) for u in range(2)]
-        nc.sync.dma_start(out=x_table_scales[SCALE_ROWS_AT:P, :].bitcast(I32), in_=x_scales[0].bitcast(I32))
+        nc.scalar.dma_start(out=x_table_scales[SCALE_ROWS_AT:P, :].bitcast(I32), in_=x_scales[0].bitcast(I32))
         nc.sync.dma_start(offs_sb[:], offs)
         nc.sync.dma_start(out=w1_raw[0][:], in_=w1_rows[:, 0:2, :])
         nc.sync.dma_start(out=w1_raw[1][:], in_=w1_rows[:, 2:4, :])
@@ -196,48 +196,59 @@ def tile_picked_deliver_gelu_po_kernel(
         out_words = as_words(out_1)
         out_codes = sb.tile([P, S], I32, name="out_codes", align_bytes=64)
         out_scale = sb.tile([P, S], U8, name="out_scale", align_bytes=64)
-        result = [sb.tile([P, PACK, CHUNK], F32, name=f"result{c}", align_bytes=64) for c in range(CHUNKS)]
+        result = [sb.tile([P, PACK, HALF], F32, name=f"result{h}", align_bytes=64) for h in range(2)]
         result_bf = [sb.tile([P, HALF, PACK], BF16, name=f"result_bf{h}", align_bytes=64) for h in range(2)]
-        for c in range(CHUNKS):
-            by_pairs = c < CHUNKS // 2
-            for u in range(2):
-                pair = slice(2 * u, 2 * u + 2)
-                acc = psum.tile([P, 2, CHUNK], F32, name=f"acc{c}_{u}", tag=f"bank{2 * c + u}")
+
+        def second_product(acc, t, tokens):
+            nc.tensor.matmul_mx(
+                out=acc,
+                lhsT=w2_codes[:, t * P : (t + 1) * P].bitcast(FP8X4),
+                lhsT_scale=w2_scale[:, t * P : (t + 1) * P],
+                rhs=z_codes[:, tokens].bitcast(FP8X4),
+                rhs_scale=z_scale[:, tokens],
+                start=True,
+                stop=True,
+            )
+
+        for h in range(2):
+            for t in range(2):
+                acc = psum.tile([P, HALF], F32, name=f"wide{h}_{t}", tag=f"bank{4 * h + t}")
+                if (h, t) == (0, 0):
+                    for c in range(2):
+                        second_product(acc[:, chunk[c]], t, chunk[c])
+                else:
+                    second_product(acc[:], t, halves[h])
+                copy = nc.vector.tensor_copy if (h, t) in BANKS_ON_VECTOR else nc.scalar.copy
+                copy(out=result[h][:, t, :], in_=acc[:])
+                if h == 0:
+                    nc.sync.dma_start(out=out_rows[:, t, halves[h]], in_=result[h][:, t, :])
+            if h == 1:
+                nc.sync.dma_start(out=out_rows[:, 0:2, halves[h]], in_=result[h][:, 0:2, :])
+            for c in range(2):
+                acc = psum.tile([P, 2, CHUNK], F32, name=f"pair{h}_{c}", tag=f"bank{4 * h + 2 + c}")
                 for e in range(2):
-                    t = 2 * u + e
-                    nc.tensor.matmul_mx(
-                        out=acc[:, e, :],
-                        lhsT=w2_codes[:, t * P : (t + 1) * P].bitcast(FP8X4),
-                        lhsT_scale=w2_scale[:, t * P : (t + 1) * P],
-                        rhs=z_codes[:, chunk[c]].bitcast(FP8X4),
-                        rhs_scale=z_scale[:, chunk[c]],
-                        start=True,
-                        stop=True,
-                    )
-                copy = nc.vector.tensor_copy if (c, u) in BANKS_ON_VECTOR else nc.scalar.copy
-                copy(out=result[c][:, pair, :], in_=acc[:])
-                if by_pairs:
-                    nc.sync.dma_start(out=out_rows[:, pair, chunk[c]], in_=result[c][:, pair, :])
-            if not by_pairs:
-                nc.sync.dma_start(out=out_rows[:, :, chunk[c]], in_=result[c][:])
+                    second_product(acc[:, e, :], 2 + e, chunk[2 * h + c])
+                nc.scalar.copy(out=result[h][:, 2:4, chunk[c]], in_=acc[:])
+            nc.sync.dma_start(out=out_rows[:, 2:4, halves[h]], in_=result[h][:, 2:4, :])
 
         def interleave(c):
             nc.vector.tensor_copy(
                 out=result_bf[c // 2][:, chunk[c % 2], :].rearrange("p (a i) t -> p a t i", i=4),
-                in_=result[c][:].rearrange("p t (a i) -> p a t i", i=4),
+                in_=result[c // 2][:, :, chunk[c % 2]].rearrange("p t (a i) -> p a t i", i=4),
             )
 
-        def quantise_out(h, part):
-            tokens = slice(h * HALF + part.start, h * HALF + part.stop)
+        def quantise_out(c):
             nc.vector.quantize_mx(
-                out=out_codes[:, tokens].bitcast(FP8X4), scales=out_scale[:, tokens], in_=result_bf[h][:, part, :].rearrange("p n t -> p (n t)")
+                out=out_codes[:, chunk[c]].bitcast(FP8X4),
+                scales=out_scale[:, chunk[c]],
+                in_=result_bf[c // 2][:, chunk[c % 2], :].rearrange("p n t -> p (n t)"),
             )
 
-        for h, parts in enumerate(([halves[0]], chunk[0:2])):
+        for h in range(2):
             interleave(2 * h)
             interleave(2 * h + 1)
-            for part in parts:
-                quantise_out(h, part)
+            quantise_out(2 * h)
+            quantise_out(2 * h + 1)
             nc.sync.dma_start(out=out_words[:, halves[h]], in_=out_codes[:, halves[h]])
         for q in range(4):
             queue = nc.scalar if q % 2 else nc.sync

@@ -124,13 +124,8 @@ def tile_picked_deliver_gelu_po_kernel(
         def deal(dealt, raw):
             nc.vector.tensor_copy(out=dealt[:].rearrange("p (t m) -> p m t", t=PACK), in_=raw[:].rearrange("p (m t) -> p m t", t=PACK))
 
-        w2_codes = sb.tile([P, N], I32, name="w2_codes", align_bytes=64)
-        deal(w2_codes, w2_raw)
-
-        z = {t: reused.tile([P, S], F32, name=f"z{t}", offset=at, align_bytes=64) for t, at in ((first, N), (second, N + 4 * S + 4 * V))}
-        z[third] = sb.tile([P, S], F32, name=f"z{third}", align_bytes=64)
-        fetched = {t: sb.tile([P, V], F32, name=f"fetched{t}", tag=f"fetched{t}", align_bytes=64) for t in ORDER[1:]}
-        fetched[first] = reused.tile([P, V], F32, name=f"fetched{first}", offset=N + 4 * S, align_bytes=64)
+        z = {t: sb.tile([P, S], F32, name=f"z{t}", align_bytes=64) for t in ORDER[:3]}
+        fetched = {t: sb.tile([P, V], F32, name=f"fetched{t}", tag=f"fetched{t}", align_bytes=64) for t in ORDER}
         message = {t: sb.tile([P, V], F32, name=f"message{t}", align_bytes=64) for t in ORDER[1:]}
         message[first] = fetched[first]
 
@@ -166,7 +161,11 @@ def tile_picked_deliver_gelu_po_kernel(
         activate(third)
         deliver(third)
         fetch(last)
-
+        w2_codes = sb.tile([P, N], U32, name="w2_codes", tag=f"fetched{third}", align_bytes=64)
+        nc.scalar.copy(
+            out=w2_codes[:].rearrange("p (t a i) -> p a t i", t=PACK, i=4),
+            in_=w2_raw[:].bitcast(U32).rearrange("p (a i t) -> p a t i", t=PACK, i=4),
+        )
         activate(last)
         deliver(last)
         w2_scale = sb.tile([P, N], U8, name="w2_scale", tag=f"fetched{last}", align_bytes=64)

from contextlib import ExitStack

import concourse.mybir as mybir

K, T, S, V, N, H = 512, 2048, 512, 256, 512, 512
FLOPS = 2 * K * H * S + 2 * H * N * S

F32 = mybir.dt.float32
BF16 = mybir.dt.bfloat16
I32 = mybir.dt.int32
U32 = mybir.dt.uint32
U16 = mybir.dt.uint16
U8 = mybir.dt.uint8
FP8X4 = mybir.dt.float8_e4m3fn_x4
GELU = mybir.ActivationFunctionType.Gelu_apprx_tanh
COPY = mybir.ActivationFunctionType.Copy

P = 128
PACK = 4
LIST_ROWS = 16
HALF = S // 2
CHUNK = 128
CHUNKS = S // CHUNK
SCALE_ROWS_AT = P - K // 32
ORDER = (2, 0, 3, 1)
BANKS_ON_VECTOR = ((0, 1),)


def as_words(packed):
    return packed[0].rearrange("p n t -> p (n t)").bitcast(I32)


def load_scale_rows(queue, tile, scales):
    for q in range(4):
        queue.dma_start(out=tile[32 * q : 32 * q + 4, :].bitcast(I32), in_=scales[0, 4 * q : 4 * q + 4, :].bitcast(I32))


def tile_picked_deliver_gelu_po_kernel(
    tc, x_words, x_scales, w1, w2_words, w2_scales, offs, src, dst, out_0, out_1, out_2
):
    nc = tc.nc
    with ExitStack() as ctx:
        sb = ctx.enter_context(tc.tile_pool(name="sb", bufs=1))
        reused = ctx.enter_context(tc.tile_pool(name="reused", bufs=1))
        psum = ctx.enter_context(tc.psum_pool(name="psum", bufs=1))

        offs_sb = sb.tile([P, S // LIST_ROWS], U16, name="offs_sb")
        src_sb = sb.tile([P, V // LIST_ROWS], U16, name="src_sb")
        dst_sb = sb.tile([P, V // LIST_ROWS], U16, name="dst_sb")
        x_table = sb.tile([P, T], I32, name="x_table", align_bytes=64)
        x_table_scales = reused.tile([P, T], U8, name="x_table_scales", offset=0, align_bytes=64)
        x_scale = sb.tile([P, S], U8, name="x_scale", align_bytes=64)

        nc.vector.memset(x_table_scales[0:96, :].bitcast(I32), 0)
        nc.vector.memset(x_table_scales[96:SCALE_ROWS_AT, :].bitcast(I32), 0)
        nc.vector.memset(x_scale[:].bitcast(I32), 0)

        w1_rows = w1.rearrange("(p j) c -> p j c", j=PACK)
        w1_raw = [sb.tile([P, 2, H], F32, name=f"w1_raw{u}", align_bytes=64) for u in range(2)]
        nc.scalar.dma_start(out=x_table_scales[SCALE_ROWS_AT:P, :].bitcast(I32), in_=x_scales[0].bitcast(I32))
        nc.sync.dma_start(offs_sb[:], offs)
        nc.sync.dma_start(out=w1_raw[0][:], in_=w1_rows[:, 0:2, :])
        nc.sync.dma_start(out=w1_raw[1][:], in_=w1_rows[:, 2:4, :])
        nc.sync.dma_start(out=x_table[:], in_=as_words(x_words))
        nc.sync.dma_start(src_sb[:], src)
        nc.sync.dma_start(dst_sb[:], dst)

        picked_scales = sb.tile([P, S], U8, name="picked_scales", align_bytes=64)
        nc.vector.tensor_copy(picked_scales[:], x_table_scales[:].indirect(offs_sb[:]))
        for q in range(4):
            rows = slice(SCALE_ROWS_AT + 4 * q, SCALE_ROWS_AT + 4 * q + 4)
            nc.scalar.dma_start(out=x_scale[32 * q : 32 * q + 4, :].bitcast(I32), in_=picked_scales[rows, :].bitcast(I32))
        w2_raw = reused.tile([P, N], I32, name="w2_raw", offset=T - 64, align_bytes=64)
        w2_raw_scales = reused.tile([P, N], U8, name="w2_raw_scales", offset=0, align_bytes=64)
        nc.sync.dma_start(out=w2_raw[:], in_=as_words(w2_words))
        nc.vector.memset(w2_raw_scales[:].bitcast(I32), 0)
        load_scale_rows(nc.sync, w2_raw_scales, w2_scales)

        w1_bf = sb.tile([P, PACK, P, PACK], BF16, name="w1_bf", align_bytes=64)
        for u in range(2):
            nc.vector.tensor_copy(
                out=w1_bf[:, :, :, 2 * u : 2 * u + 2].rearrange("p t m j -> p m j t"),
                in_=w1_raw[u][:].rearrange("p j (m t) -> p m j t", t=PACK),
            )
        w1_codes = sb.tile([P, H], U32, name="w1_codes", align_bytes=64)
        w1_scale = sb.tile([P, H], U8, name="w1_scale", align_bytes=64)
        nc.vector.quantize_mx(out=w1_codes[:].bitcast(FP8X4), scales=w1_scale[:], in_=w1_bf[:].rearrange("p t m j -> p (t m j)"))

        x_codes = [sb.tile([P, HALF], U32, name=f"x_codes{h}", align_bytes=64) for h in range(2)]
        for start, count in ((0, HALF), (HALF, CHUNK), (HALF + CHUNK, CHUNK)):
            h, at = divmod(start, HALF)
            offsets = offs_sb[:, start // LIST_ROWS : (start + count) // LIST_ROWS]
            nc.vector.tensor_copy(x_codes[h][:, at : at + count], x_table[:].bitcast(U32).indirect(offsets))

        def first_product(acc, t, tokens):
            h, at = divmod(tokens.start, HALF)
            nc.tensor.matmul_mx(
                out=acc,
                lhsT=w1_codes[:, t * P : (t + 1) * P].bitcast(FP8X4),
                lhsT_scale=w1_scale[:, t * P : (t + 1) * P],
                rhs=x_codes[h][:, at : at + tokens.stop - tokens.start].bitcast(FP8X4),
                rhs_scale=x_scale[:, tokens],
                start=True,
                stop=True,
            )

        first, second, third, last = ORDER
        halves = [slice(h * HALF, (h + 1) * HALF) for h in range(2)]
        chunk = [slice(c * CHUNK, (c + 1) * CHUNK) for c in range(CHUNKS)]
        first_parts = [halves[0], chunk[2], chunk[3]]
        first_banks = [psum.tile([P, part.stop - part.start], F32, name=f"y_first{i}", tag=f"bank{i}") for i, part in enumerate(first_parts)]
        second_banks = [psum.tile([P, HALF], F32, name=f"y_second{h}", tag=f"bank{3 + h}") for h in range(2)]
        last_bank = psum.tile([P, S], F32, name="y_last", tag="bank6")
        first_product(first_banks[0][:], first, first_parts[0])
        first_product(second_banks[0][:], second, halves[0])
        for bank, part in zip(first_banks[1:], first_parts[1:]):
            first_product(bank[:], first, part)
        first_product(second_banks[1][:], second, halves[1])

        first_gelu = sb.tile([P, S], F32, name="first_gelu", tag="first_gelu", align_bytes=64)
        for bank, part in zip(first_banks, first_parts):
            nc.scalar.activation(first_gelu[:, part], bank[:], GELU)

        def deal(dealt, raw):
            nc.vector.tensor_copy(out=dealt[:].rearrange("p (t m) -> p m t", t=PACK), in_=raw[:].rearrange("p (m t) -> p m t", t=PACK))

        z = {t: sb.tile([P, S], F32, name=f"z{t}", align_bytes=64) for t in ORDER[:3]}
        fetched = {t: sb.tile([P, V], F32, name=f"fetched{t}", tag=f"fetched{t}", align_bytes=64) for t in ORDER}
        message = {t: sb.tile([P, V], F32, name=f"message{t}", align_bytes=64) for t in ORDER[1:]}
        message[first] = fetched[first]

        def fetch(t):
            nc.scalar.activation(fetched[t][:], z[t][:].indirect(src_sb[:]), COPY)

        def activate(t):
            nc.scalar.activation(message[t][:], fetched[t][:], GELU)

        def deliver(t):
            nc.vector.tensor_copy(z[t][:].indirect(dst_sb[:]), message[t][:])

        nc.vector.tensor_copy(out=z[second][:, halves[0]], in_=second_banks[0][:])
        nc.vector.tensor_copy(fetched[first][:], first_gelu[:].indirect(src_sb[:]))
        z[last] = sb.tile([P, S], F32, name=f"z{last}", tag="first_gelu", align_bytes=64)
        for bank, part in zip(first_banks, first_parts):
            nc.scalar.copy(out=z[first][:, part], in_=bank[:])
        deliver(first)
        third_banks = [psum.tile([P, HALF], F32, name="y_third0", tag="bank0")]
        first_product(third_banks[0][:], third, halves[0])
        for half in halves:
            first_product(last_bank[:, half], last, half)
        nc.scalar.copy(out=z[second][:, halves[1]], in_=second_banks[1][:])
        nc.scalar.copy(out=z[third][:, halves[0]], in_=third_banks[0][:])
        third_banks.append(psum.tile([P, HALF], F32, name="y_third1", tag="bank4"))
        first_product(third_banks[1][:], third, halves[1])
        fetch(second)
        nc.scalar.copy(out=z[third][:, halves[1]], in_=third_banks[1][:])
        activate(second)
        deliver(second)
        fetch(third)
        nc.scalar.copy(out=z[last][:], in_=last_bank[:])
        activate(third)
        deliver(third)
        fetch(last)
        w2_codes = sb.tile([P, N], U32, name="w2_codes", tag=f"fetched{third}", align_bytes=64)
        nc.scalar.copy(
            out=w2_codes[:].rearrange("p (t a i) -> p a t i", t=PACK, i=4),
            in_=w2_raw[:].bitcast(U32).rearrange("p (a i t) -> p a t i", t=PACK, i=4),
        )
        activate(last)
        deliver(last)
        w2_scale = sb.tile([P, N], U8, name="w2_scale", tag=f"fetched{last}", align_bytes=64)
        deal(w2_scale, w2_raw_scales)

        z_bf = sb.tile([P, S, PACK], BF16, name="z_bf", tag=f"fetched{second}", align_bytes=64)

        def round_on_gpsimd(out, values):
            nc.gpsimd.tensor_scalar(out=out, in0=values, scalar1=1.0, scalar2=0.0, op0=mybir.AluOpType.mult, op1=mybir.AluOpType.add)

        for t in (first, second):
            round_on_gpsimd(z_bf[:, :, t : t + 2], z[t][:].rearrange("p (n o) -> p n o", o=1).to_broadcast([P, S, 2]))
        for half in halves:
            nc.scalar.copy(out=z_bf[:, half, third], in_=z[third][:, half])
        for c, part in enumerate(chunk):
            copy = nc.vector.tensor_copy if c < CHUNKS // 2 else nc.scalar.copy
            copy(out=z_bf[:, part, last], in_=z[last][:, part])

        z_codes = sb.tile([P, S], U32, name="z_codes", align_bytes=64)
        z_scale = sb.tile([P, S], U8, name="z_scale", align_bytes=64)
        for part in (chunk[0], chunk[1], halves[1]):
            nc.vector.quantize_mx(
                out=z_codes[:, part].bitcast(FP8X4), scales=z_scale[:, part], in_=z_bf[:, part, :].rearrange("p n t -> p (n t)")
            )

        out_rows = out_0.rearrange("(p t) n -> p t n", t=PACK)
        out_words = as_words(out_1)
        out_codes = sb.tile([P, S], I32, name="out_codes", align_bytes=64)
        out_scale = sb.tile([P, S], U8, name="out_scale", align_bytes=64)
        result = [sb.tile([P, PACK, HALF], F32, name=f"result{h}", align_bytes=64) for h in range(2)]
        result_bf = [sb.tile([P, HALF, PACK], BF16, name=f"result_bf{h}", align_bytes=64) for h in range(2)]

        def second_product(acc, t, tokens):
            nc.tensor.matmul_mx(
                out=acc,
                lhsT=w2_codes[:, t * P : (t + 1) * P].bitcast(FP8X4),
                lhsT_scale=w2_scale[:, t * P : (t + 1) * P],
                rhs=z_codes[:, tokens].bitcast(FP8X4),
                rhs_scale=z_scale[:, tokens],
                start=True,
                stop=True,
            )

        for h in range(2):
            for t in range(2):
                acc = psum.tile([P, HALF], F32, name=f"wide{h}_{t}", tag=f"bank{4 * h + t}")
                if (h, t) == (0, 0):
                    for c in range(2):
                        second_product(acc[:, chunk[c]], t, chunk[c])
                else:
                    second_product(acc[:], t, halves[h])
                copy = nc.vector.tensor_copy if (h, t) in BANKS_ON_VECTOR else nc.scalar.copy
                copy(out=result[h][:, t, :], in_=acc[:])
                if h == 0:
                    nc.sync.dma_start(out=out_rows[:, t, halves[h]], in_=result[h][:, t, :])
            if h == 1:
                nc.sync.dma_start(out=out_rows[:, 0:2, halves[h]], in_=result[h][:, 0:2, :])
            for c in range(2):
                acc = psum.tile([P, 2, CHUNK], F32, name=f"pair{h}_{c}", tag=f"bank{4 * h + 2 + c}")
                for e in range(2):
                    second_product(acc[:, e, :], 2 + e, chunk[2 * h + c])
                nc.scalar.copy(out=result[h][:, 2:4, chunk[c]], in_=acc[:])
            nc.sync.dma_start(out=out_rows[:, 2:4, halves[h]], in_=result[h][:, 2:4, :])

        def interleave(c):
            nc.vector.tensor_copy(
                out=result_bf[c // 2][:, chunk[c % 2], :].rearrange("p (a i) t -> p a t i", i=4),
                in_=result[c // 2][:, :, chunk[c % 2]].rearrange("p t (a i) -> p a t i", i=4),
            )

        def quantise_out(c):
            nc.vector.quantize_mx(
                out=out_codes[:, chunk[c]].bitcast(FP8X4),
                scales=out_scale[:, chunk[c]],
                in_=result_bf[c // 2][:, chunk[c % 2], :].rearrange("p n t -> p (n t)"),
            )

        for h in range(2):
            interleave(2 * h)
            interleave(2 * h + 1)
            quantise_out(2 * h)
            quantise_out(2 * h + 1)
            nc.sync.dma_start(out=out_words[:, halves[h]], in_=out_codes[:, halves[h]])
        for q in range(4):
            queue = nc.scalar if q % 2 else nc.sync
            queue.dma_start(out=out_2[0, 4 * q : 4 * q + 4, :].bitcast(I32), in_=out_scale[32 * q : 32 * q + 4, :].bitcast(I32))
